import numpy as np, ml_dtypes
CORES = [24,25,26,27,28,29,30,31]
N = 8
import mx_ref
BF = ml_dtypes.bfloat16
def gentries(a):
    return np.ascontiguousarray(a.reshape(8, 16, -1).transpose(0, 2, 1)).reshape(8, -1)
def gtable(e):
    e = np.asarray(e); return np.ascontiguousarray(e.reshape(8, -1, 16).transpose(0, 2, 1)).reshape(128, -1).astype(np.int32)
def gcols(t, e):
    v = np.concatenate([t.reshape(8, 16, -1, 4), np.zeros((8, 16, 1, 4), BF)], axis=2)
    return np.ascontiguousarray(np.stack([v[g][:, e[g]] for g in range(8)])).reshape(128, -1)
def tile(rs):
    return np.stack(rs, axis=2).reshape(128, -1).astype(BF)
def pick(q, e):
    c = np.concatenate([q[0].reshape(128, -1, 4), np.zeros((128, 1, 4), np.uint8)], axis=1); s = np.concatenate([q[1], np.ones((16, 1), np.uint8)], axis=1)
    return (np.ascontiguousarray(c[:, e].reshape(128, -1)), np.ascontiguousarray(s[:, e]))
def join(*qs):
    return (np.concatenate([q[0] for q in qs], axis=1), np.concatenate([q[1] for q in qs], axis=1))
def put(q, e, v):
    c, s = q[0].reshape(128, -1, 4).copy(), q[1].copy(); c[:, e] = v[0].reshape(128, -1, 4); s[:, e] = v[1]
    return (c.reshape(128, -1), s)
def pk(c, s):
    return (np.ascontiguousarray(c), mx_ref.live(s))
def emit(q):
    return q[0], q[1]
def packed(v, rng):
    q = [mx_ref.quantize(np.ascontiguousarray(v[r])) for r in range(N)]
    return np.stack([a for a, b in q]), np.stack([mx_ref.plane(b, rng) for a, b in q])
def values_of_codes():
    e, c = np.zeros((128, 128, 4), np.float32), np.zeros((128, 2, 4), np.uint8)
    e[np.arange(128), np.arange(128), 0] = 1
    c[:127, :, 0] = np.arange(256).reshape(2, 128).T[:127]
    return mx_ref.matmul(mx_ref.quantize(e.reshape(128, 512).astype(BF)), (c.reshape(128, 8), np.full((16, 2), 127, np.uint8))).T.reshape(-1).astype(np.float64)
CODE_VALUE, SCALE_VALUE = values_of_codes(), 2.0 ** (np.arange(256) - 127.0)
def decode(q):
    return (CODE_VALUE[q[0]].reshape(16, 8, -1, 4) * SCALE_VALUE[q[1]][:, None, :, None] + 0.0).reshape(128, -1).astype(np.float32)
def f(rng, *shape):
    return mx_ref.flush((rng.standard_normal(shape, dtype=np.float32) * np.exp2(rng.integers(-2, 3, shape[:-1] + (1,)))).astype(BF))
def wide(rng, *shape, cols=0):
    v = rng.standard_normal(shape, dtype=np.float32) * np.exp2(rng.integers(-12, 13, shape)).astype(np.float32)
    if cols: v *= np.repeat(np.exp2(rng.integers(-cols, cols + 1, shape[:-2] + (1, shape[-1] // 4))) * (rng.random(shape[:-2] + (1, shape[-1] // 4)) > 0.0625), 4, axis=-1).astype(np.float32)
    return mx_ref.flush(v.astype(BF))
C, I = 256, 16
DIST = [1, 2, 4]
def big(v):
    v = v.astype(np.float32)
    v[np.abs(v) < np.float32(2.0 ** -16)] = 0
    return v.astype(BF)
def alike(t):
    return np.stack([t] * N)
def lists(t):
    return {"li": np.stack([gtable(t[0][r]) for r in range(N)]), "ri": np.stack([gtable(t[1][r]) for r in range(N)])}
def drawn(rng):
    return lists(rng.integers(0, I, (2, N, 8, C)))
def layers(rng):
    return big(f(rng, 128, 2048)).reshape(8, 16, 4, 8, 16, 4)
def weights(rng, w):
    c, s = packed(alike(np.ascontiguousarray(w).reshape(128, 2048)), rng)
    return {"wc": c, "ws": alike(s[0])}
def setup_inputs(rng):
    return {"x": big(f(rng, N, 128, 4 * C)), "u": alike(np.array(f(rng, 128, 512))), "mid": alike(big(f(rng, 128, 4 * I * I))), "v": np.array(f(rng, N, 128, 512)), **drawn(rng), **weights(rng, layers(rng))}
def scorer(rng):
    u = np.array(f(rng, 128, 512)).reshape(128, 128, 4)
    u[:, ::16] = 0
    return u
def setup_inputs_few(rng):
    d = setup_inputs(rng)
    x = d["x"].reshape(N, 8, 16, C, 4)
    e = rng.permutation(N)
    for r in range(N):
        k = rng.permutation(np.array([0, 1, 2, 3, C // 2 - 1, C // 2, C - 1, C]))
        if r == e[0]: k[:] = 0
        if r == e[1]: k[:] = C
        for g in range(8):
            c = (-rng.integers(0, 2, C)).astype(np.float32)
            c[rng.permutation(C)[:k[g]]] = 1
            x[r, g, 0, :, 0] = c.astype(BF)
    u = scorer(rng)
    for h in range(0, 128, 16): u[h, h, 0] = 1.0
    t = rng.integers(0, I, (2, N, 8, C))
    t[:, e[0]] = I - 1
    t[:, e[1]] = 0
    t[:, e[2]] = rng.integers(0, I, (2, 8, 1))
    w = layers(rng)
    w[:, :, :, :, 0] = 0
    return {"x": x.reshape(N, 128, 4 * C), "u": alike(u.reshape(128, 512)), "mid": d["mid"], "v": d["v"], **lists(t), **weights(rng, w)}
def setup_inputs_near(rng):
    d = setup_inputs(rng)
    x = d["x"].reshape(N, 8, 16, C, 4)
    x[:, :, :8] = 0
    o = rng.permutation(N) % 4
    for r in range(N):
        s = rng.integers(-1, 2, (8, C)).astype(np.float32)
        if o[r] % 2 == 1: s = s[:, np.arange(C) // 16]
        if o[r] < 2: s = s * np.float32(2.0 ** -30)
        for g in rng.permutation(8)[:4]: s[g, rng.integers(C)] = 2.0 ** 29 * rng.choice([-1.0, 1.0])
        x[r, :, 0, :, 0] = s.astype(BF)
    u = scorer(rng)
    small = rng.permutation(8)[:4]
    for g in range(8): u[16 * g, 16 * g, 0] = 2.0 ** -30 if g in small else 1.0
    m = np.array(d["mid"][0]).reshape(8, 16, I * I, 4)
    m[:, :8] = 0
    m[:, 0, :, 0] = 2.0 ** -28
    w = layers(rng)
    w[:, :8] = 0
    w[:, :, :, :, :8] = 0
    return {"x": x.reshape(N, 128, 4 * C), "u": alike(u.reshape(128, 512)), "mid": alike(m.reshape(128, 4 * I * I)), "v": d["v"], **drawn(rng), **weights(rng, w)}
def setup_inputs_fine(rng):
    d = setup_inputs(rng)
    x = d["x"].reshape(N, 8, 16, C, 4)
    x[:, :, :8] = 0
    n = rng.integers(1, 15, (N, 8, C))
    o = rng.permutation(N) % 3
    a = np.stack([n, n + rng.integers(-1, 2, (N, 8, C))], axis=-1) * np.exp2(o - 17.0)[:, None, None, None]
    x[:, :, 0, :, :2] = a.astype(np.float32).astype(BF)
    x[:, :, 1, :, 0] = 1.96875
    x[:, :, 8, :, 0] = 1.0
    u = scorer(rng)
    for h in range(0, 128, 16):
        u[h, h, 0] = 1.0
        u[h, h, 1] = -1.0
    m = np.array(d["mid"][0]).reshape(8, 16, I * I, 4)
    m[:, :8] = 0
    m[:, 8, :, 0] = 1.0
    w = layers(rng)
    w[:, :, :, :, :9] = 0
    w[np.arange(8), 8, 0, np.arange(8), 1, 0] = -1.0
    return {"x": x.reshape(N, 128, 4 * C), "u": alike(u.reshape(128, 512)), "mid": alike(m.reshape(128, 4 * I * I)), "v": d["v"], **drawn(rng), **weights(rng, w)}
def setup_inputs_huge(rng):
    d = setup_inputs(rng)
    h = rng.permutation(8)
    x = -0.98 - 0.02 * rng.random((N, 8, 16, C, 4))
    x[:, h[4:]] = (0.75 + 0.1 * rng.random((N, 4, 16, C, 4))) * rng.choice([-1.0, 1.0], (N, 4, 1, C, 1))
    m = (0.75 + 0.1 * rng.random((8, 16, I * I, 4))) * rng.choice([-1.0, 1.0], (8, 1, I * I, 1))
    u = scorer(rng)
    for g in range(8):
        a = 16 * int(rng.choice(h[4:]))
        u[a:a + 16, 16 * g] = (2.0 ** 30 * (1 - 0.1 * rng.random((16, 4))) * rng.choice([-1.0, 1.0])).astype(np.float32).astype(BF)
    w = np.zeros((128, 4, 128, 4), np.float32)
    i = np.arange(128)
    for b in range(4): w[i, b, i, b] = -1
    return {"x": (2.0 ** 30 * x).astype(np.float32).astype(BF).reshape(N, 128, 4 * C), "u": alike(u.reshape(128, 512)), "mid": alike((2.0 ** 30 * m).astype(np.float32).astype(BF).reshape(128, 4 * I * I)), "v": d["v"], **drawn(rng), **weights(rng, w.astype(BF))}
def setup_inputs_spread(rng):
    d = setup_inputs(rng)
    d["x"] = big(wide(rng, N, 128, 4 * C, cols=6))
    d["mid"] = alike(big(wide(rng, 128, 4 * I * I)))
    return d
def check_inputs(d):
    b = []
    for k in ("x", "u", "mid", "v"):
        a = np.abs(d[k].astype(np.float32))
        if not (np.isfinite(a).all() and ((a == 0) | (a >= 2.0 ** -30) & (a <= 2.0 ** 30)).all()): b.append("a value of " + k)
    for k in ("li", "ri"):
        if not ((d[k] >= 0) & (d[k] < I)).all(): b.append("an entry of " + k)
    for k in ("u", "mid", "wc", "ws"):
        if (d[k] != d[k][:1]).any(): b.append(k + " isn't the same on all ranks")
    if ((d["wc"] & 0x7F) == 0x7F).any(): b.append("a code of wc that is no number")
    none, least, most = [emit(mx_ref.quantize(np.full((128, 16), k, np.float32).astype(BF)))[1][0, 0] for k in (0.0, 2.0 ** -30, 2.0 ** 30)]
    for r in range(N):
        s = mx_ref.live(d["ws"][r])
        if ((s != none) & ((s < least) | (s > most))).any(): b.append("a scale of ws")
    return b
def reference(x, u, mid, v, li, ri, wc, ws):
    qu = [mx_ref.quantize(u[r]) for r in range(N)]
    lay = [pk(wc[r], ws[r]) for r in range(N)]
    third = [decode(mx_ref.quantize(mid[r])).astype(BF) for r in range(N)]
    state = [mx_ref.quantize(x[r]) for r in range(N)]
    left = [gentries(li[r]) for r in range(N)]
    right = [gentries(ri[r]) for r in range(N)]
    mix = np.arange(C).reshape(2, C // 2).T.reshape(-1)
    for d in DIST:
        made, outl, outr = [], [], []
        for r in range(N):
            s = mx_ref.matmul(qu[r], state[r])[::16]
            o = np.argsort(~(s > 0), axis=1, kind="stable")
            l, h = o[:, ::2], o[:, 1::2]
            full = decode(state[r]).astype(BF)
            most = np.maximum(gcols(full, l).astype(np.float32), gcols(full, h).astype(np.float32))
            n = I * np.take_along_axis(right[r], l, axis=1) + np.take_along_axis(left[r], h, axis=1)
            z = mx_ref.quantize(((most + gcols(third[r], n).astype(np.float32)) * np.float32(0.5)).astype(BF))
            made.append(mx_ref.quantize(tile([mx_ref.matmul(pick(lay[r], np.arange(128 * b, 128 * b + 128)), z) * np.float32(0.03125) + most[:, b::4] for b in range(4)])))
            outl.append(np.take_along_axis(left[r], l, axis=1))
            outr.append(np.take_along_axis(right[r], h, axis=1))
        for r in range(N):
            e = (r - d) % N
            state[r] = pick(join(made[e], made[r]), mix)
            left[r] = np.concatenate([outl[e], outl[r]], axis=1)[:, mix]
            right[r] = np.concatenate([outr[e], outr[r]], axis=1)[:, mix]
    y, lr = np.zeros((N, 128, C), np.float32), np.zeros((N, 8, 2 * C), np.float32)
    oc, osc = np.zeros((N, 128, 4 * C), np.uint8), np.zeros((N, 16, C), np.uint8)
    for r in range(N):
        y[r] = mx_ref.matmul(mx_ref.quantize(v[r]), state[r])
        lr[r] = np.concatenate([left[r], right[r]], axis=1)
        oc[r], osc[r] = emit(state[r])
    return {"y": y, "lr": lr, "oc": oc, "osc": osc}

@@ -1,0 +1,413 @@
+from concourse.mybir import dt, AluOpType, ActivationFunctionType
+
+BF, F32, I32, U16, U8, MX = "bfloat16", "float32", "int32", "uint16", "uint8", "float8_e4m3fn_x4"
+DIST = [1, 2, 4]
+FAR = float(2 ** 80)
+XN = 160
+
+SCRATCH = {
+    "xs": ("sbuf", [128, 1024], BF), "us": ("sbuf", [128, 512], BF), "ms": ("sbuf", [128, 1024], BF),
+    "vs": ("sbuf", [128, 512], BF), "lis": ("sbuf", [128, 16], I32), "ris": ("sbuf", [128, 16], I32),
+    "wq": ("sbuf", [128, 512], MX), "wp": ("sbuf", [128, 512], U8),
+    "qu": ("sbuf", [128, 128], MX), "pu": ("sbuf", [128, 128], U8),
+    "qg": ("sbuf", [128, 128], MX), "pg": ("sbuf", [128, 128], U8),
+    "qv": ("sbuf", [128, 128], MX), "pv": ("sbuf", [128, 128], U8),
+    "qm": ("sbuf", [128, 256], MX), "pm": ("sbuf", [128, 256], U8),
+    "ip": ("sbuf", [128, 1], I32), "bi": ("sbuf", [128, 2], I32), "cf": ("sbuf", [128, 4], F32),
+    "rn": ("sbuf", [128, 128], BF), "dg": ("sbuf", [128, 128], BF), "jr": ("sbuf", [128, 48], F32),
+    "ia": ("sbuf", [128, 64], BF), "tq": ("sbuf", [128, 64], BF),
+    "eb": ("sbuf", [128, 516], BF), "qe": ("sbuf", [128, 512], MX), "pe": ("sbuf", [128, 512], U8),
+    "kk": ("sbuf", [128, 384], BF),
+    "xc": ("sbuf", [128, 4 * XN], BF), "qx": ("sbuf", [128, XN], MX), "px": ("sbuf", [128, XN], U8),
+    "jt": ("sbuf", [128, 64], F32), "ft": ("sbuf", [128, 192], F32), "tf": ("sbuf", [128, 192], F32),
+    "uo": ("sbuf", [128, 8], U16), "so": ("sbuf", [128, 16], U16), "go": ("sbuf", [128, 8], U16),
+    "fo": ("sbuf", [128, 16], U16), "lo": ("sbuf", [128, 16], U16),
+    "w0": ("sbuf", [128, 512], BF), "w1": ("sbuf", [128, 512], BF),
+    "qw": ("sbuf", [128, 256], MX), "pw": ("sbuf", [128, 256], U8),
+    "own": ("sbuf", [128, 32], F32), "ab": ("sbuf", [128, 32], F32), "mn": ("sbuf", [128, 16], F32),
+    "po": ("sbuf", [128, 16], U16), "yw": ("sbuf", [128, 512], BF), "ty": ("sbuf", [128, 512], BF),
+    "src": ("sbuf", [128, 256], BF), "srt": ("sbuf", [128, 288], BF), "tt": ("sbuf", [128, 512], BF),
+    "gn": ("sbuf", [128, 32], F32), "lh": ("sbuf", [128, 32], U16), "no": ("sbuf", [128, 8], U16),
+    "fh": ("sbuf", [128, 1024], BF), "mh": ("sbuf", [128, 1024], BF), "lf": ("sbuf", [128, 512], BF),
+    "ph": ("sbuf", [128, 512], BF), "p32": ("sbuf", [128, 512], BF), "zt": ("sbuf", [128, 512], BF),
+    "qz": ("sbuf", [128, 128], MX), "pz": ("sbuf", [128, 128], U8),
+    "v32": ("sbuf", [128, 512], BF), "vt": ("sbuf", [128, 512], BF),
+    "qf": ("sbuf", [128, 256], MX), "pf": ("sbuf", [128, 256], U8),
+    "yo": ("sbuf", [128, 256], F32), "lro": ("sbuf", [128, 256], F32),
+}
+for _k in range(4):
+    SCRATCH["q%d" % _k] = ("sbuf", [128, 256], MX)
+    SCRATCH["p%d" % _k] = ("sbuf", [128, 256], U8)
+for _k in range(1, 4):
+    SCRATCH["iw%d" % _k] = ("sbuf", [128, 64], BF)
+for _k in range(1, 3):
+    SCRATCH["cs%d" % _k] = ("sbuf", [128, 32], F32)
+    SCRATCH["cr%d" % _k] = ("sbuf", [128, 32], F32)
+for _k in range(8):
+    SCRATCH["b%d" % _k] = ("psum", [128, 512], F32)
+
+POOL = {"v": 56, "s": 30, "t": 20, "g": 12, "d": 14}
+ARRIVE = ["ri1", "ri2", "ri3", "rq1", "rq2", "rq3", "rp1", "rp2", "rp3", "rc1", "rc2"]
+SEMAPHORES = ["%s%d" % (q, i) for q in POOL for i in range(POOL[q])] + ARRIVE + ["sent"]
+
+
+def emit(ops, queues, T):
+    size, last = {}, {}
+    for i, o in enumerate(ops):
+        size[o["grp"]] = size.get(o["grp"], 0) + o["inc"]
+        last[o["grp"]] = i
+    writer, readers, known, seen, waits, wanted, before = {}, {}, {}, {}, [], set(), []
+    for i, o in enumerate(ops):
+        need = []
+        for t in o["r"] + o["w"]:
+            if t in writer:
+                need.append(writer[t])
+        for t in o["w"]:
+            need += readers.get(t, [])
+        kn = known.setdefault(o["q"], set())
+        mine = []
+        for x in sorted(set(need), key=lambda x: -last[x]):
+            if x != o["grp"] and x not in kn:
+                assert last[x] < i, (x, o["grp"])
+                mine.append(x)
+                kn.add(x)
+                kn.update(seen[x])
+        waits.append(mine)
+        wanted.update(mine)
+        before.append(set(kn))
+        seen.setdefault(o["grp"], set()).update(kn)
+        for t in o["r"]:
+            if o["hold"]:
+                readers.setdefault(t, []).append(o["grp"])
+        for t in o["w"]:
+            writer[t] = o["grp"]
+            readers[t] = []
+    turn, count, user, place = {}, {}, {}, {}
+    for i, o in enumerate(ops):
+        x = o["grp"]
+        if o["sem"] is not None:
+            place[x] = (o["sem"], size[x])
+            continue
+        e = queues[o["q"]]
+        for y in waits[i]:
+            e.wait_ge(T.sem[place[y][0]], place[y][1])
+        if o["fn"] is None:
+            continue
+        if x in wanted and x not in place:
+            pool = o["pool"]
+            n = turn.get(pool, 0)
+            turn[pool] = n + 1
+            name = "%s%d" % (pool, n % POOL[pool])
+            if name in user and user[name] not in before[i]:
+                e.wait_ge(T.sem[name], count[name])
+            user[name] = x
+            count[name] = count.get(name, 0) + size[x]
+            place[x] = (name, count[name])
+        ins = o["fn"]()
+        if x in wanted:
+            ins.then_inc(T.sem[place[x][0]], o["inc"])
+
+
+def rank_program(g, core, T, topo):
+    rank = T.rank_of(core)
+    if rank is None:
+        return
+    n_ranks = len(T.cores)
+    A, ACT = AluOpType, ActivationFunctionType
+    vec, sca, ten = g.vector, g.scalar, g.tensor
+    queues = {"v": vec, "s": sca, "t": ten, "g": g, "y": g.sync}
+    ops = []
+
+    def op(q, fn, r, w, grp=None, pool=None, inc=1, hold=True, sem=None):
+        ops.append({"q": q, "fn": fn, "r": list(r), "w": list(w), "grp": grp or "op%d" % len(ops),
+                    "pool": pool or q, "inc": inc, "hold": hold, "sem": sem})
+
+    def dma(q, out, in_, r, w, grp=None):
+        op(q, lambda: queues[q].dma_start(out, in_), r, w, grp, pool="d", inc=16)
+
+    def ts(out, in0, s1, s2, o0, o1, r, w, grp=None):
+        if s2 is None:
+            op("v", lambda: vec.tensor_scalar(out, in0, s1, None, o0), r, w, grp)
+        else:
+            op("v", lambda: vec.tensor_scalar(out, in0, s1, s2, o0, o1), r, w, grp)
+
+    def tt(out, in0, in1, o, r, w, grp=None):
+        op("v", lambda: vec.tensor_tensor(out, in0, in1, o), r, w, grp)
+
+    def cp(out, in_, r, w, grp=None):
+        op("v", lambda: vec.tensor_copy(out, in_), r, w, grp)
+
+    def tr(out, in_, r, w, grp=None):
+        op("v", lambda: vec.transpose(out, in_), r, w, grp)
+
+    def fill(out, c, w, grp=None):
+        op("v", lambda: vec.memset(out, c), [], w, grp)
+
+    def quant(q, p, in_, r, w, grp=None):
+        op("v", lambda: vec.quantize_mx(q, p, in_), r, w, grp)
+
+    def act(out, in_, r, w, scale=None, bias=None, grp=None):
+        if bias is not None:
+            op("s", lambda: sca.activation(out, in_, ACT.Identity, bias=bias), r, w, grp)
+        elif scale is not None:
+            op("s", lambda: sca.activation(out, in_, ACT.Copy, scale=scale), r, w, grp)
+        else:
+            op("s", lambda: sca.activation(out, in_, ACT.Copy), r, w, grp)
+
+    def mm(out, lq, lp, rq, rp, r, w, start=True, stop=True, grp=None):
+        op("t", lambda: ten.matmul_mx(out, lq, lp, rq, rp, start, stop), r, w, grp)
+
+    def iota(out, pattern, base, cm, w, grp=None, whole=False):
+        if whole:
+            op("g", lambda: g.iota(out, pattern, base, cm), [], w, grp)
+        else:
+            op("g", lambda: g.iota(out, pattern, base, cm, allow_small_or_imprecise_dtypes=True), [], w, grp)
+
+    sent = [0]
+
+    def send(k, out, in_, sem, r):
+        dst = T.cores[(rank + DIST[k - 1]) % n_ranks]
+        rid, pid, _ = topo.addr(dst)
+        mask = topo.mask(core, dst)
+        sent[0] += len(topo.engines(core, dst))
+        op("g", lambda: g.remote_dma(out, in_, T.sem[sem], T.sem.sent, pid, rid, mask), r, [], hold=False)
+
+    def arrive(k, sem, w):
+        src = T.cores[(rank - DIST[k - 1]) % n_ranks]
+        op("x", None, [], w, inc=len(topo.engines(src, core)), sem=sem)
+
+    bank = [T["b%d" % k] for k in range(8)]
+    col = lambda c: T.cf[:, c:c + 1]
+    words = lambda v: v.bitcast(dt.uint32)
+    raw = lambda v: v.bitcast(dt.uint8)
+
+    def half(t, h):
+        return t[:, 128 * h:128 * h + 128]
+
+    dma("y", T.us[:], T.u[:], [], ["us"])
+    dma("s", T.lis[:], T.li[:], [], ["lis"], "lists")
+    dma("s", T.ris[:], T.ri[:], [], ["ris"], "lists")
+    dma("y", T.xs[:, 0:512], T.x[:, 0:512], [], ["xs0"])
+    dma("y", T.xs[:, 512:1024], T.x[:, 512:1024], [], ["xs1"])
+    dma("y", T.ms[:], T.mid[:], [], ["ms"])
+    dma("y", T.wp[:], T.ws[:], [], ["wp"], "layer")
+    dma("y", raw(T.wq[:]), T.wc[:], [], ["wq"], "layer")
+    dma("y", T.vs[:], T.v[:], [], ["vs"])
+
+    iota(T.ip[:], [[0, 1]], 0, 1, ["ip"], whole=True)
+    iota(T.jr[:, 0:16], [[16, 16]], 0, 0, ["jr0"])
+    iota(T.ia[:, 0:32], [[16, 8], [-16, 2], [-16, 2]], 16, -1, ["ia0"], "ia")
+    iota(T.ia[:, 32:64], [[16, 8], [-16, 2], [0, 2]], 16, -1, ["ia1"], "ia")
+    iota(T.rn[:], [[0, 8], [1, 16]], 0, 0, ["rn"])
+    iota(T.dg[:], [[1, 128]], 0, -1, ["dg"])
+    for h in range(2):
+        for t, pat, base in ((0, [[0, 2], [32, 4], [128, 2]], 0), (1, [[255, 2], [32, 4], [128, 2]], 2),
+                             (2, [[32, 4], [128, 2], [0, 2]], 1), (3, [[32, 4], [128, 2], [0, 2]], 258)):
+            c = 32 * t + 16 * h
+            iota(T.ft[:, c:c + 16], pat, base + 16 * h, 0, ["ft%d%d" % (t, h)], "ft")
+    iota(T.ft[:, 128:160], [[0, 2], [1, 8], [128, 2]], 0, 0, ["ft4"], "fu")
+    iota(T.ft[:, 160:192], [[16, 2], [1, 8], [256, 2]], 0, 0, ["ft5"], "fu")
+    iota(T.jr[:, 16:32], [[1, 2], [32, 8]], 0, 0, ["jr1"], "fu")
+    iota(T.jr[:, 32:48], [[32, 8], [8, 2]], 0, 0, ["jr2"], "fu")
+
+    blk = lambda k: T.xc[:, 32 * k:32 * k + 32]
+    fill(T.eb[:], 0.0, ["eb"])
+    fill(T.jt[:], 0.0, ["jt"], "z1")
+    fill(T.xc[:, 96:160], 0.0, ["xz0"], "z1")
+    fill(blk(1), 1.0, ["x1"], "z1")
+    fill(blk(6), 1.0, ["x6"], "z1")
+    act(T.yw[:], T.eb[:, 0:512], ["eb"], ["yw"], grp="z2")
+    act(T.w0[:, 3:512:4], T.eb[:, 0:128], ["eb"], ["w0z"], grp="z2")
+    act(T.w1[:, 3:512:4], T.eb[:, 0:128], ["eb"], ["w1z"], grp="z2")
+    act(T.xc[:, 512:4 * XN], T.eb[:, 0:4 * XN - 512], ["eb"], ["xz1"], grp="z2")
+    act(T.srt[:], T.eb[:, 0:288], ["eb"], ["srt"], grp="z2")
+    ts(T.bi[:, 0:1], T.ip[:], 15, None, A.bitwise_and, None, ["ip"], ["bi0"], "bi")
+    ts(T.bi[:, 1:2], T.ip[:], 31, None, A.bitwise_and, None, ["ip"], ["bi1"], "bi")
+    cp(T.uo[:], T.jr[:, 0:8], ["jr0"], ["uo"])
+    cp(T.cf[:, 0:2], T.bi[:], ["bi0", "bi1"], ["cf01"])
+    ts(blk(8), T.ia[:, 0:32], 0.0, None, A.is_gt, None, ["ia0"], ["x8"], "xa")
+    ts(blk(13), T.ia[:, 32:64], 0.0, None, A.is_gt, None, ["ia1"], ["x13"], "xa")
+    ts(blk(10), T.ia[:, 0:32], 0.0, None, A.is_le, None, ["ia0"], ["x10"], "xa")
+    ts(blk(15), T.ia[:, 32:64], 0.0, None, A.is_le, None, ["ia1"], ["x15"], "xa")
+    ts(col(2), col(0), 2.0, -256.0, A.mult, A.add, ["cf01"], ["cf2"], "cf")
+    ts(col(3), col(1), col(0), 2.0, A.subtract, A.mult, ["cf01"], ["cf3"], "cf")
+    tt(T.tq[:, 0:32], blk(13), blk(8), A.subtract, ["x8", "x13"], ["tq0"])
+    ts(T.so[:], T.jr[:, 0:16], 2.0, col(1), A.mult, A.add, ["jr0", "cf01"], ["so"])
+    ts(T.jt[:, 16:32], T.jr[:, 0:16], col(0), -256.0, A.add, A.add, ["jr0", "cf01", "jt"], ["jt0"])
+    ts(T.tq[:, 32:64], T.tq[:, 0:32], 256.0, None, A.mult, None, ["tq0"], ["tq1"])
+    for t, o in enumerate((A.is_le, A.not_equal, A.is_ge)):
+        ts(T.kk[:, 128 * t:128 * t + 128], T.rn[:], col(0), FAR, o, A.mult, ["rn", "cf01"], ["kk%d" % t], "kk")
+    tt(blk(0), blk(8), T.tq[:, 32:64], A.subtract, ["x8", "tq1"], ["x0"], "xb")
+    tt(blk(2), blk(15), T.tq[:, 32:64], A.add, ["x15", "tq1"], ["x2"], "xb")
+    act(T.yw[:, 0:512:32], T.jr[:, 0:16], ["jr0", "cf01", "yw"], ["yc0"], bias=col(0), grp="yc")
+    act(T.yw[:, 16:512:32], T.jr[:, 0:16], ["jr0", "cf01", "yw"], ["yc1"], bias=col(0), grp="yc")
+    for k in (5, 9, 12):
+        act(blk(k), blk(0), ["x0"], ["x%d" % k], grp="xd")
+    for k in (7, 11, 14):
+        act(blk(k), blk(2), ["x2"], ["x%d" % k], grp="xd")
+    ts(T.eb[:, 3:515:4], T.dg[:], 0.0, None, A.is_equal, None, ["dg", "eb"], ["eb"])
+    for b in range(4):
+        quant(half(T.qe, b), half(T.pe, b), T.eb[:, 3 - b:515 - b], ["eb"], ["qe%d" % b], "qe")
+
+    def rows(r):
+        tr(T.ty[:], T.yw[:], r + ["yw", "yc0", "yc1"], ["ty"])
+
+    quant(T.qu[:], T.pu[:], T.us[:], ["us"], ["qu"])
+    for h in range(2):
+        cp(T.yw[:, 1 + 16 * h:512:32], T.lis[:], ["lis", "yw"], ["ya%d" % h], "y0")
+        ts(T.yw[:, 2 + 16 * h:512:32], T.ris[:], 16.0, None, A.mult, None, ["ris", "yw"], ["yb%d" % h], "y0")
+    cp(words(T.qg[:]), words(T.qu[:]).indirect(T.uo[:, 0:8]), ["qu", "uo"], ["qg"])
+    act(T.pg[:], T.pu[:].indirect(T.uo[:, 0:8]), ["qu", "uo"], ["pg"])
+    rows(["ya0", "ya1", "yb0", "yb1"])
+    xall = ["x%d" % k for k in (0, 1, 2, 5, 6, 7, 8, 9, 10, 11, 12, 13, 14, 15)] + ["xz0", "xz1"]
+
+    def scores(k, h, bk, r):
+        mm(bank[bk][:, 0:128], half(T["q%d" % k], h), half(T["p%d" % k], h), T.qg[:], T.pg[:],
+           r + ["qg", "pg"], ["b%d" % bk])
+
+    def flags(k, i, bk):
+        w = T["w%d" % i]
+        for t in range(3):
+            tt(w[:, t:512:4], bank[bk][:, 0:128], T.kk[:, 128 * t:128 * t + 128], A.is_gt,
+               ["b%d" % bk, "kk%d" % t], ["w%d%d" % (i, t)], "fl%d%d" % (k, i))
+
+    def packed(i):
+        quant(half(T.qw, i), half(T.pw, i), T["w%d" % i][:], ["w%d%d" % (i, t) for t in range(3)] + ["w%dz" % i], ["qw%d" % i])
+
+    def count(i, c, start, stop, grp):
+        mm(bank[2][:, 0:128], half(T.qw, i), half(T.pw, i), T.qx[:, c:c + 128], T.px[:, c:c + 128],
+           ["qw%d" % i, "qx"], ["b2"], start, stop, grp)
+
+    def unpack(q, p, n, r):
+        for b in range(4):
+            mm(bank[4 + b][:, 0:n], half(T.qe, b), half(T.pe, b), q, p, r + ["qe%d" % b], ["b%d" % (4 + b)])
+
+    def keep(dst, c, n, w):
+        for b in range(4):
+            act(dst[:, 256 * b + c:256 * b + c + n], bank[4 + b][:, 0:n], ["b%d" % (4 + b)],
+                [x % b for x in w], scale=0.5)
+
+    quant(half(T.q0, 0), half(T.p0, 0), T.xs[:, 0:512], ["xs0"], ["q00"])
+    scores(0, 0, 0, ["q00"])
+    quant(T.qx[:], T.px[:], T.xc[:], xall, ["qx"])
+    act(T.src[:], T.ty[:].indirect(T.so[:]), ["ty", "so"], ["src"])
+    flags(0, 0, 0)
+    quant(half(T.q0, 1), half(T.p0, 1), T.xs[:, 512:1024], ["xs1"], ["q01"])
+    scores(0, 1, 1, ["q01"])
+    unpack(T.q0[:], T.p0[:], 256, ["q00", "q01"])
+    keep(T.fh, 0, 256, ["f%d0", "f%d1"])
+    packed(0)
+    count(0, 0, True, False, "ab0")
+    tr(T.tf[:, 0:128], T.ft[:, 0:128], ["ft00"], ["tf"])
+    flags(0, 1, 1)
+    packed(1)
+    count(1, 32, False, True, "ab0")
+    quant(T.qm[:], T.pm[:], T.ms[:], ["ms"], ["qm"])
+    unpack(T.qm[:], T.pm[:], 256, ["qm"])
+    keep(T.mh, 0, 256, ["m%d"])
+    tt(T.ab[:], bank[2][:, 0:32], T.jt[:, 0:32], A.add, ["b2", "jt0", "jt"], ["ab"])
+
+    for k in range(1, 4):
+        q, p, iw = T["q%d" % k], T["p%d" % k], T["iw%d" % k]
+        if k == 1:
+            cp(T.go[:, 0:4:2], T.tf[:, 0:64:32], ["tf"], ["go0"], "go")
+        tt(T.mn[:], T.ab[:, 0:16], T.ab[:, 16:32], A.min, ["ab"], ["mn"])
+        if k == 1:
+            cp(T.go[:, 4:6], T.tf[:, 64:128:32], ["tf"], ["go"], "go")
+        ts(T.po[:], T.mn[:], col(3), 256.0, A.add, A.add, ["mn", "cf3"], ["po"])
+        cp(T.srt[:].indirect(T.po[:]), T.src[:], ["po", "src"], ["srt"])
+        for j in range(2):
+            for s in (2 * j, 2 * j + 1):
+                a = (0, 32, 1, 33)[s]
+                tr(half(T.tt, s), T.srt[:, a:a + 255:2], ["srt"], ["tt%d" % s], "tt%d%d" % (k, j))
+            ts(T.lh[:, 16 * j:16 * j + 16], T.tt[:, 256 * j:256 * j + 256].indirect(T.go[:, 0:1]), 0.0, None, A.add, None,
+               ["tt%d" % (2 * j), "tt%d" % (2 * j + 1), "go"], ["lh%d" % j])
+        tts = ["tt%d" % s for s in range(4)]
+        cp(T.gn[:, 0:16], T.tt[:].indirect(T.go[:, 2:3]), tts + ["go"], ["gn0"])
+        for b in range(4):
+            act(half(T.lf, b), T.fh[:, 256 * b:256 * b + 256].indirect(T.lh[:, 0:8]),
+                ["lh0", "f%d0" % b, "f%d1" % b], ["lf%d" % b])
+        act(iw[:, 32:64], T.tt[:].indirect(T.go[:, 4:6]), tts + ["go"], ["iw%d1" % k])
+        send(k, iw[:, 0:32], iw[:, 32:64], "ri%d" % k, ["iw%d1" % k])
+
+        def larger(b):
+            tt(half(T.ph, b), T.fh[:, 256 * b:256 * b + 256].indirect(T.lh[:, 16:24]), half(T.lf, b), A.max,
+               ["lh1", "lf%d" % b, "f%d0" % b, "f%d1" % b], ["ph%d" % b])
+            act(half(T.p32, b), half(T.ph, b), ["ph%d" % b], ["p32%d" % b], scale=64.0)
+
+        def middle(b):
+            tt(T.zt[:, b:512:4], T.mh[:, 256 * b:256 * b + 256].indirect(T.no[:]), half(T.ph, b), A.add,
+               ["no", "m%d" % b, "ph%d" % b], ["zt%d" % b], "zt%d" % k)
+
+        larger(0)
+        tt(T.gn[:, 16:24], T.gn[:, 0:8], T.gn[:, 8:16], A.add, ["gn0"], ["gn1"])
+        larger(1)
+        cp(T.no[:], T.gn[:, 16:24], ["gn1"], ["no"])
+        larger(2), middle(0), larger(3), middle(1), middle(2), middle(3)
+        quant(T.qz[:], T.pz[:], T.zt[:], ["zt%d" % b for b in range(4)], ["qz"])
+        for b in range(4):
+            mm(bank[4 + b][:, 0:128], half(T.wq, b), half(T.wp, b), T.qz[:], T.pz[:], ["wq", "wp", "qz"], ["b%d" % (4 + b)])
+        for b in range(4):
+            tt(half(T.v32, b), bank[4 + b][:, 0:128], half(T.p32, b), A.add, ["b%d" % (4 + b), "p32%d" % b], ["v32%d" % b])
+            if b < 2:
+                act(T.vt[:, b:512:4], half(T.v32, b), ["v32%d" % b], ["vt%d" % b], scale=0.03125, grp="vt%d" % k)
+        for b in (2, 3):
+            ts(T.vt[:, b:512:4], half(T.v32, b), 0.03125, None, A.mult, None, ["v32%d" % b], ["vt%d" % b], "vu%d" % k)
+        quant(half(q, 1), half(p, 1), T.vt[:], ["vt%d" % b for b in range(4)], ["q%d1" % k])
+        send(k, raw(half(q, 0)), raw(half(q, 1)), "rq%d" % k, ["q%d1" % k])
+        send(k, half(p, 0), half(p, 1), "rp%d" % k, ["q%d1" % k])
+        arrive(k, "ri%d" % k, ["iw%d0" % k])
+        arrive(k, "rq%d" % k, ["aq%d" % k])
+        arrive(k, "rp%d" % k, ["ap%d" % k])
+
+        def relist(last):
+            for h in range(2):
+                c = 256 * h
+                cp(T.yw[:, c + 1:c + 256:16], iw[:, 32 * h:32 * h + 16], ["iw%d%d" % (k, h)], ["ya%d" % h], "y%d" % k)
+                ts(T.yw[:, c + 2:c + 256:16], iw[:, 32 * h + 16:32 * h + 32], 0.0625 if last else 1.0, None, A.mult, None,
+                   ["iw%d%d" % (k, h)], ["yb%d" % h], "y%d" % k)
+            rows(["ya0", "ya1", "yb0", "yb1"])
+
+        if k < 3:
+            cs, cr = T["cs%d" % k], T["cr%d" % k]
+            scores(k, 1, 0, ["q%d1" % k])
+            unpack(half(q, 1), half(p, 1), 128, ["q%d1" % k])
+            flags(k, 0, 0)
+            packed(0)
+            count(0, 0, True, True, None)
+            cp(cs[:], bank[2][:, 96:128], ["b2"], ["cs%d" % k])
+            send(k, cr[:], cs[:], "rc%d" % k, ["cs%d" % k])
+            arrive(k, "rc%d" % k, ["cr%d" % k])
+            keep(T.fh, 128, 128, ["f%d1"])
+            if k == 1:
+                ts(T.jt[:, 48:64], T.jr[:, 16:32], col(2), None, A.add, None, ["jr1", "cf2", "jt"], ["jt1"])
+                tr(T.tf[:, 128:192], T.ft[:, 128:192], ["ft4"], ["tg"])
+            tt(T.own[:], bank[2][:, 64:96], T.jt[:, 32:64], A.add, ["b2", "jt1", "jt"], ["own"])
+            relist(False)
+            act(T.src[:], T.ty[:].indirect(T.so[:]), ["ty", "so"], ["src"])
+            if k == 1:
+                quant(T.qv[:], T.pv[:], T.vs[:], ["vs"], ["qv"])
+                ts(T.fo[:], T.jr[:, 0:16], 0.5, T.tf[:, 128:129], A.mult, A.add, ["jr0", "tg"], ["fo"])
+                ts(T.lo[:], T.jr[:, 32:48], T.tf[:, 160:161], None, A.add, None, ["jr2", "tg"], ["lo"])
+            unpack(half(q, 0), half(p, 0), 128, ["aq%d" % k, "ap%d" % k])
+            keep(T.fh, 0, 128, ["f%d0"])
+            tt(T.ab[:], T.own[:], cr[:], A.add, ["own", "cr%d" % k], ["ab"])
+        else:
+            mm(bank[0][:, 0:128], T.qv[:], T.pv[:], half(q, 1), half(p, 1), ["qv", "q31"], ["b0"])
+            relist(True)
+            cp(T.yo[:, 1:256:2], bank[0][:, 0:128], ["b0"], ["yo1"])
+            act(T.lro[:], T.ty[:].indirect(T.lo[:]), ["ty", "lo"], ["lro"])
+            dma("y", T.lr[:, 0:256], T.lro[1:128:16, :], ["lro"], ["o0"], "out0")
+            dma("y", T.lr[:, 256:512], T.lro[2:128:16, :], ["lro"], ["o1"], "out0")
+            mm(bank[1][:, 0:128], T.qv[:], T.pv[:], half(q, 0), half(p, 0), ["qv", "aq3", "ap3"], ["b1"])
+            for h in range(2):
+                cp(words(half(T.qf, h)), words(q[:]).indirect(T.fo[:, 8 * h:8 * h + 8]), ["aq3", "q31", "fo"], ["qf%d" % h])
+                act(half(T.pf, h), p[:].indirect(T.fo[:, 8 * h:8 * h + 8]), ["ap3", "q31", "fo"], ["pf%d" % h], grp="pf")
+                dma("y", T.oc[:, 512 * h:512 * h + 512], raw(half(T.qf, h)), ["qf%d" % h], ["o2%d" % h], "out1")
+            cp(T.yo[:, 0:256:2], bank[1][:, 0:128], ["b1"], ["yo0"])
+            dma("y", T.y[:], T.yo[:], ["yo0", "yo1"], ["o3"], "out1")
+            for j in range(4):
+                dma("s", T.osc[4 * j:4 * j + 4, :], T.pf[32 * j:32 * j + 4, :], ["pf0", "pf1"], ["o4%d" % j], "out2")
+    op("y", None, ["o0", "o3", "o40"], [])
+    emit(ops, queues, T)
+    g.wait_ge(T.sem.sent, sent[0])

@@ -3,28 +3,27 @@ from concourse.mybir import dt, AluOpType, ActivationFunctionType
 BF, F32, I32, U16, U8, MX = "bfloat16", "float32", "int32", "uint16", "uint8", "float8_e4m3fn_x4"
 DIST = [1, 2, 4]
 FAR = float(2 ** 80)
-XN = 160
+LOW = -1024.0
 
 SCRATCH = {
     "xs": ("sbuf", [128, 1024], BF), "us": ("sbuf", [128, 512], BF), "ms": ("sbuf", [128, 1024], BF),
-    "vs": ("sbuf", [128, 512], BF), "lis": ("sbuf", [128, 16], I32), "ris": ("sbuf", [128, 16], I32),
+    "vs": ("sbuf", [128, 512], BF), "s0": ("sbuf", [128, 256], I32),
     "wq": ("sbuf", [128, 512], MX), "wp": ("sbuf", [128, 512], U8),
     "qu": ("sbuf", [128, 128], MX), "pu": ("sbuf", [128, 128], U8),
     "qg": ("sbuf", [128, 128], MX), "pg": ("sbuf", [128, 128], U8),
     "qv": ("sbuf", [128, 128], MX), "pv": ("sbuf", [128, 128], U8),
     "qm": ("sbuf", [128, 256], MX), "pm": ("sbuf", [128, 256], U8),
-    "ip": ("sbuf", [128, 1], I32), "bi": ("sbuf", [128, 2], I32), "cf": ("sbuf", [128, 4], F32),
-    "rn": ("sbuf", [128, 128], BF), "dg": ("sbuf", [128, 128], BF), "jr": ("sbuf", [128, 48], F32),
-    "ia": ("sbuf", [128, 64], BF), "tq": ("sbuf", [128, 64], BF),
+    "ip": ("sbuf", [128, 2], I32), "bi": ("sbuf", [128, 4], I32), "cf": ("sbuf", [128, 8], F32),
+    "rn": ("sbuf", [128, 128], BF), "dg": ("sbuf", [128, 128], BF), "jr": ("sbuf", [128, 96], F32),
+    "tq": ("sbuf", [128, 16], BF),
     "eb": ("sbuf", [128, 516], BF), "qe": ("sbuf", [128, 512], MX), "pe": ("sbuf", [128, 512], U8),
-    "kk": ("sbuf", [128, 384], BF),
-    "xc": ("sbuf", [128, 4 * XN], BF), "qx": ("sbuf", [128, XN], MX), "px": ("sbuf", [128, XN], U8),
-    "jt": ("sbuf", [128, 64], F32), "ft": ("sbuf", [128, 192], F32), "tf": ("sbuf", [128, 192], F32),
+    "kk": ("sbuf", [128, 768], BF),
+    "xc": ("sbuf", [128, 512], BF), "qx": ("sbuf", [128, 128], MX), "px": ("sbuf", [128, 128], U8),
+    "jt": ("sbuf", [128, 48], F32), "ft": ("sbuf", [128, 128], F32), "tf": ("sbuf", [128, 128], F32),
     "uo": ("sbuf", [128, 8], U16), "so": ("sbuf", [128, 16], U16), "go": ("sbuf", [128, 8], U16),
     "fo": ("sbuf", [128, 16], U16), "lo": ("sbuf", [128, 16], U16),
-    "w0": ("sbuf", [128, 512], BF), "w1": ("sbuf", [128, 512], BF),
-    "qw": ("sbuf", [128, 256], MX), "pw": ("sbuf", [128, 256], U8),
-    "own": ("sbuf", [128, 32], F32), "ab": ("sbuf", [128, 32], F32), "mn": ("sbuf", [128, 16], F32),
+    "wf": ("sbuf", [128, 1024], BF), "qw": ("sbuf", [128, 256], MX), "pw": ("sbuf", [128, 256], U8),
+    "hi": ("sbuf", [128, 16], F32), "own": ("sbuf", [128, 48], F32), "sc": ("sbuf", [128, 48], F32),
     "po": ("sbuf", [128, 16], U16), "yw": ("sbuf", [128, 512], BF), "ty": ("sbuf", [128, 512], BF),
     "src": ("sbuf", [128, 256], BF), "srt": ("sbuf", [128, 288], BF), "tt": ("sbuf", [128, 512], BF),
     "gn": ("sbuf", [128, 32], F32), "lh": ("sbuf", [128, 32], U16), "no": ("sbuf", [128, 8], U16),
@@ -41,8 +40,8 @@ for _k in range(4):
 for _k in range(1, 4):
     SCRATCH["iw%d" % _k] = ("sbuf", [128, 64], BF)
 for _k in range(1, 3):
-    SCRATCH["cs%d" % _k] = ("sbuf", [128, 32], F32)
-    SCRATCH["cr%d" % _k] = ("sbuf", [128, 32], F32)
+    SCRATCH["cs%d" % _k] = ("sbuf", [128, 48], BF)
+    SCRATCH["cr%d" % _k] = ("sbuf", [128, 48], BF)
 for _k in range(8):
     SCRATCH["b%d" % _k] = ("psum", [128, 512], F32)
 
@@ -140,6 +139,9 @@ def rank_program(g, core, T, topo):
     def tr(out, in_, r, w, grp=None):
         op("v", lambda: vec.transpose(out, in_), r, w, grp)
 
+    def scan(out, d0, d1, r, w):
+        op("v", lambda: vec.tensor_tensor_scan(out, d0, d1, 0.0, A.add, A.max), r, w)
+
     def fill(out, c, w, grp=None):
         op("v", lambda: vec.memset(out, c), [], w, grp)
 
@@ -148,7 +150,7 @@ def rank_program(g, core, T, topo):
 
     def act(out, in_, r, w, scale=None, bias=None, grp=None):
         if bias is not None:
-            op("s", lambda: sca.activation(out, in_, ACT.Identity, bias=bias), r, w, grp)
+            op("s", lambda: sca.activation(out, in_, ACT.Identity, bias=bias, scale=1.0 if scale is None else scale), r, w, grp)
         elif scale is not None:
             op("s", lambda: sca.activation(out, in_, ACT.Copy, scale=scale), r, w, grp)
         else:
@@ -185,150 +187,156 @@ def rank_program(g, core, T, topo):
         return t[:, 128 * h:128 * h + 128]
 
     dma("y", T.us[:], T.u[:], [], ["us"])
-    dma("s", T.lis[:], T.li[:], [], ["lis"], "lists")
-    dma("s", T.ris[:], T.ri[:], [], ["ris"], "lists")
     dma("y", T.xs[:, 0:512], T.x[:, 0:512], [], ["xs0"])
     dma("y", T.xs[:, 512:1024], T.x[:, 512:1024], [], ["xs1"])
     dma("y", T.ms[:], T.mid[:], [], ["ms"])
+
+    iota(T.ip[:], [[2048, 2]], 0, 16, ["ip"], whole=True)
+    iota(T.dg[:], [[1, 128]], 0, -1, ["dg"])
+    iota(T.jr[:, 48:80], [[0, 4], [1, 8]], 0, 0, ["jr3"])
+    iota(T.jr[:, 0:16], [[16, 16]], 0, 0, ["jr0"])
+    iota(T.rn[:], [[0, 8], [1, 16]], 0, 0, ["rn"])
+    iota(T.s0[:], [[1, 16], [16, 16]], 0, 0, ["s0"], whole=True)
+    dma("y", T.s0[1:128:16, :], T.li[:], ["s0"], ["s0a"], "lists")
+    dma("y", T.s0[2:128:16, :], T.ri[:], ["s0"], ["s0b"], "lists")
     dma("y", T.wp[:], T.ws[:], [], ["wp"], "layer")
     dma("y", raw(T.wq[:]), T.wc[:], [], ["wq"], "layer")
     dma("y", T.vs[:], T.v[:], [], ["vs"])
-
-    iota(T.ip[:], [[0, 1]], 0, 1, ["ip"], whole=True)
-    iota(T.jr[:, 0:16], [[16, 16]], 0, 0, ["jr0"])
-    iota(T.ia[:, 0:32], [[16, 8], [-16, 2], [-16, 2]], 16, -1, ["ia0"], "ia")
-    iota(T.ia[:, 32:64], [[16, 8], [-16, 2], [0, 2]], 16, -1, ["ia1"], "ia")
-    iota(T.rn[:], [[0, 8], [1, 16]], 0, 0, ["rn"])
-    iota(T.dg[:], [[1, 128]], 0, -1, ["dg"])
+    iota(T.ft[:, 0:32], [[16, 2], [32, 8], [128, 2]], 0, 0, ["ft0"], "ft")
     for h in range(2):
-        for t, pat, base in ((0, [[0, 2], [32, 4], [128, 2]], 0), (1, [[255, 2], [32, 4], [128, 2]], 2),
-                             (2, [[32, 4], [128, 2], [0, 2]], 1), (3, [[32, 4], [128, 2], [0, 2]], 258)):
-            c = 32 * t + 16 * h
-            iota(T.ft[:, c:c + 16], pat, base + 16 * h, 0, ["ft%d%d" % (t, h)], "ft")
-    iota(T.ft[:, 128:160], [[0, 2], [1, 8], [128, 2]], 0, 0, ["ft4"], "fu")
-    iota(T.ft[:, 160:192], [[16, 2], [1, 8], [256, 2]], 0, 0, ["ft5"], "fu")
+        iota(T.ft[:, 32 + 16 * h:48 + 16 * h], [[32, 4], [128, 2], [0, 2]], 16 * h, 0, ["ft1%d" % h], "ft")
+    iota(T.jr[:, 80:82], [[257, 2]], 1, 0, ["jr4"], "ft")
+    iota(T.ft[:, 64:96], [[0, 2], [1, 8], [128, 2]], 0, 0, ["ft4"], "fu")
+    iota(T.ft[:, 96:128], [[16, 2], [1, 8], [256, 2]], 0, 0, ["ft5"], "fu")
     iota(T.jr[:, 16:32], [[1, 2], [32, 8]], 0, 0, ["jr1"], "fu")
     iota(T.jr[:, 32:48], [[32, 8], [8, 2]], 0, 0, ["jr2"], "fu")
 
-    blk = lambda k: T.xc[:, 32 * k:32 * k + 32]
+    x1 = lambda kind, t: T.xc[:, 4 * kind + t:128:8]
+    x2 = lambda kind, t, a=0, b=32: T.xc[:, 128 + 12 * a + 4 * kind + t:128 + 12 * b:12]
     fill(T.eb[:], 0.0, ["eb"])
-    fill(T.jt[:], 0.0, ["jt"], "z1")
-    fill(T.xc[:, 96:160], 0.0, ["xz0"], "z1")
-    fill(blk(1), 1.0, ["x1"], "z1")
-    fill(blk(6), 1.0, ["x6"], "z1")
-    act(T.yw[:], T.eb[:, 0:512], ["eb"], ["yw"], grp="z2")
-    act(T.w0[:, 3:512:4], T.eb[:, 0:128], ["eb"], ["w0z"], grp="z2")
-    act(T.w1[:, 3:512:4], T.eb[:, 0:128], ["eb"], ["w1z"], grp="z2")
-    act(T.xc[:, 512:4 * XN], T.eb[:, 0:4 * XN - 512], ["eb"], ["xz1"], grp="z2")
-    act(T.srt[:], T.eb[:, 0:288], ["eb"], ["srt"], grp="z2")
-    ts(T.bi[:, 0:1], T.ip[:], 15, None, A.bitwise_and, None, ["ip"], ["bi0"], "bi")
-    ts(T.bi[:, 1:2], T.ip[:], 31, None, A.bitwise_and, None, ["ip"], ["bi1"], "bi")
-    cp(T.uo[:], T.jr[:, 0:8], ["jr0"], ["uo"])
-    cp(T.cf[:, 0:2], T.bi[:], ["bi0", "bi1"], ["cf01"])
-    ts(blk(8), T.ia[:, 0:32], 0.0, None, A.is_gt, None, ["ia0"], ["x8"], "xa")
-    ts(blk(13), T.ia[:, 32:64], 0.0, None, A.is_gt, None, ["ia1"], ["x13"], "xa")
-    ts(blk(10), T.ia[:, 0:32], 0.0, None, A.is_le, None, ["ia0"], ["x10"], "xa")
-    ts(blk(15), T.ia[:, 32:64], 0.0, None, A.is_le, None, ["ia1"], ["x15"], "xa")
-    ts(col(2), col(0), 2.0, -256.0, A.mult, A.add, ["cf01"], ["cf2"], "cf")
-    ts(col(3), col(1), col(0), 2.0, A.subtract, A.mult, ["cf01"], ["cf3"], "cf")
-    tt(T.tq[:, 0:32], blk(13), blk(8), A.subtract, ["x8", "x13"], ["tq0"])
-    ts(T.so[:], T.jr[:, 0:16], 2.0, col(1), A.mult, A.add, ["jr0", "cf01"], ["so"])
-    ts(T.jt[:, 16:32], T.jr[:, 0:16], col(0), -256.0, A.add, A.add, ["jr0", "cf01", "jt"], ["jt0"])
-    ts(T.tq[:, 32:64], T.tq[:, 0:32], 256.0, None, A.mult, None, ["tq0"], ["tq1"])
-    for t, o in enumerate((A.is_le, A.not_equal, A.is_ge)):
-        ts(T.kk[:, 128 * t:128 * t + 128], T.rn[:], col(0), FAR, o, A.mult, ["rn", "cf01"], ["kk%d" % t], "kk")
-    tt(blk(0), blk(8), T.tq[:, 32:64], A.subtract, ["x8", "tq1"], ["x0"], "xb")
-    tt(blk(2), blk(15), T.tq[:, 32:64], A.add, ["x15", "tq1"], ["x2"], "xb")
-    act(T.yw[:, 0:512:32], T.jr[:, 0:16], ["jr0", "cf01", "yw"], ["yc0"], bias=col(0), grp="yc")
-    act(T.yw[:, 16:512:32], T.jr[:, 0:16], ["jr0", "cf01", "yw"], ["yc1"], bias=col(0), grp="yc")
-    for k in (5, 9, 12):
-        act(blk(k), blk(0), ["x0"], ["x%d" % k], grp="xd")
-    for k in (7, 11, 14):
-        act(blk(k), blk(2), ["x2"], ["x%d" % k], grp="xd")
+    fill(T.xc[:], 0.0, ["xc"])
+    ts(T.bi[:, 0:1], T.ip[:, 0:1], 255, None, A.bitwise_and, None, ["ip"], ["bi0"], "bi")
+    ts(T.bi[:, 1:3], T.ip[:], 8, None, A.arith_shift_right, None, ["ip"], ["bi1"], "bi")
+    ts(T.bi[:, 3:4], T.ip[:, 0:1], 4, 16, A.arith_shift_right, A.bitwise_and, ["ip"], ["bi2"], "bi")
     ts(T.eb[:, 3:515:4], T.dg[:], 0.0, None, A.is_equal, None, ["dg", "eb"], ["eb"])
-    for b in range(4):
+    cp(T.cf[:, 0:4], T.bi[:], ["bi0"], ["cf"])
+    quant(half(T.qe, 0), half(T.pe, 0), T.eb[:, 3:515], ["eb"], ["qe0"], "qe")
+    ts(x2(1, 2), T.jr[:, 48:80], col(1), None, A.is_gt, None, ["jr3", "cf", "xc"], ["xu"], "xa")
+    ts(x2(1, 0), T.jr[:, 48:80], col(1), None, A.is_equal, None, ["jr3", "cf", "xc"], ["xe"], "xa")
+    for b in range(1, 4):
         quant(half(T.qe, b), half(T.pe, b), T.eb[:, 3 - b:515 - b], ["eb"], ["qe%d" % b], "qe")
-
-    def rows(r):
-        tr(T.ty[:], T.yw[:], r + ["yw", "yc0", "yc1"], ["ty"])
+    zero = T.xc[:, 3:128:8]
+    act(x1(1, 0), zero, ["xc"], ["xb0"], bias=1.0, grp="xb")
+    act(x1(0, 2), zero, ["xc"], ["xb1"], bias=1.0, grp="xb")
+    act(x1(0, 0), zero, ["xc"], ["xb2"], bias=-1.0, grp="xb")
+    act(x2(0, 2), x2(1, 2), ["xu"], ["xb3"], scale=-1.0, bias=1.0, grp="xb")
+    act(x2(0, 0), x2(1, 0), ["xe"], ["xb4"], scale=-1.0, grp="xb")
+    act(x2(0, 1, 8, 24), x2(1, 0, 8, 24), ["xe"], ["xb5"], scale=-256.0, grp="xb")
+    act(x2(0, 1, 24, 32), x2(1, 0, 24, 32), ["xe"], ["xb6"], scale=-1.0, grp="xb")
+    act(x2(1, 1, 24, 32), x2(1, 0, 24, 32), ["xe"], ["xb7"], grp="xb")
+    act(T.wf[:, 3:1024:4], T.eb[:, 0:256], ["eb"], ["wz"])
+    act(T.srt[:], T.eb[:, 0:288], ["eb"], ["srt"])
+    ts(x1(1, 1), T.jr[:, 0:16], col(0), None, A.is_gt, None, ["jr0", "cf", "xc"], ["xt"], "xd")
+    ts(T.tq[:], T.jr[:, 0:16], col(0), -256.0, A.is_equal, A.mult, ["jr0", "cf"], ["tq"], "xd")
+    cp(T.uo[:], T.jr[:, 0:8], ["jr0"], ["uo"])
+    for h in range(2):
+        for t, o in enumerate((A.is_le, A.not_equal)):
+            ts(half(T.kk, 2 * h + t), T.rn[:], col(1 + h), FAR, o, A.mult, ["rn", "cf"], ["kk%d" % (2 * h + t)], "kk%d" % h)
+        if h == 0:
+            tt(x1(0, 1), T.tq[:], x1(1, 1), A.subtract, ["tq", "xt"], ["xv"])
+    act(T.jt[:, 0:32:2], zero, ["xc"], ["jt0"], bias=LOW, grp="jt")
+    act(T.jt[:, 1:32:2], T.rn[:, 0:16], ["rn", "cf"], ["jt1"], bias=col(0), grp="jt")
 
     quant(T.qu[:], T.pu[:], T.us[:], ["us"], ["qu"])
-    for h in range(2):
-        cp(T.yw[:, 1 + 16 * h:512:32], T.lis[:], ["lis", "yw"], ["ya%d" % h], "y0")
-        ts(T.yw[:, 2 + 16 * h:512:32], T.ris[:], 16.0, None, A.mult, None, ["ris", "yw"], ["yb%d" % h], "y0")
+    quant(T.qx[:], T.px[:], T.xc[:], ["xc", "xu", "xb0", "xt", "xv"], ["qx"])
     cp(words(T.qg[:]), words(T.qu[:]).indirect(T.uo[:, 0:8]), ["qu", "uo"], ["qg"])
     act(T.pg[:], T.pu[:].indirect(T.uo[:, 0:8]), ["qu", "uo"], ["pg"])
-    rows(["ya0", "ya1", "yb0", "yb1"])
-    xall = ["x%d" % k for k in (0, 1, 2, 5, 6, 7, 8, 9, 10, 11, 12, 13, 14, 15)] + ["xz0", "xz1"]
+    quant(half(T.q0, 0), half(T.p0, 0), T.xs[:, 0:512], ["xs0"], ["q00"])
 
     def scores(k, h, bk, r):
         mm(bank[bk][:, 0:128], half(T["q%d" % k], h), half(T["p%d" % k], h), T.qg[:], T.pg[:],
            r + ["qg", "pg"], ["b%d" % bk])
 
-    def flags(k, i, bk):
-        w = T["w%d" % i]
-        for t in range(3):
-            tt(w[:, t:512:4], bank[bk][:, 0:128], T.kk[:, 128 * t:128 * t + 128], A.is_gt,
-               ["b%d" % bk, "kk%d" % t], ["w%d%d" % (i, t)], "fl%d%d" % (k, i))
+    def flags(k, i, bk, kk, slots=(2, 0, 1)):
+        grp = "fl%d%d" % (k, i)
+        for t in slots:
+            w = T.wf[:, 512 * i + t:512 * i + 512:4]
+            if t == 2:
+                ts(w, bank[bk][:, 0:128], 0.0, None, A.is_gt, None, ["b%d" % bk], ["w%d2" % i], grp)
+            else:
+                tt(w, bank[bk][:, 0:128], half(T.kk, kk + t), A.is_gt, ["b%d" % bk, "kk%d" % (kk + t)], ["w%d%d" % (i, t)], grp)
 
     def packed(i):
-        quant(half(T.qw, i), half(T.pw, i), T["w%d" % i][:], ["w%d%d" % (i, t) for t in range(3)] + ["w%dz" % i], ["qw%d" % i])
+        quant(half(T.qw, i), half(T.pw, i), T.wf[:, 512 * i:512 * i + 512], ["w%d%d" % (i, t) for t in range(3)] + ["wz"], ["qw%d" % i])
 
-    def count(i, c, start, stop, grp):
-        mm(bank[2][:, 0:128], half(T.qw, i), half(T.pw, i), T.qx[:, c:c + 128], T.px[:, c:c + 128],
-           ["qw%d" % i, "qx"], ["b2"], start, stop, grp)
+    def count(i, start, stop, grp):
+        mm(bank[2][:, 0:128], half(T.qw, i), half(T.pw, i), T.qx[:], T.px[:], ["qw%d" % i, "qx"], ["b2"], start, stop, grp)
 
-    def unpack(q, p, n, r):
-        for b in range(4):
-            mm(bank[4 + b][:, 0:n], half(T.qe, b), half(T.pe, b), q, p, r + ["qe%d" % b], ["b%d" % (4 + b)])
+    def unpack(b, bk, q, p, n, r):
+        mm(bank[bk][:, 0:n], half(T.qe, b), half(T.pe, b), q, p, r + ["qe%d" % b], ["b%d" % bk])
 
-    def keep(dst, c, n, w):
-        for b in range(4):
-            act(dst[:, 256 * b + c:256 * b + c + n], bank[4 + b][:, 0:n], ["b%d" % (4 + b)],
-                [x % b for x in w], scale=0.5)
+    def keep(b, bk, dst, c, n, w):
+        act(dst[:, 256 * b + c:256 * b + c + n], bank[bk][:, 0:n], ["b%d" % bk], [x % b for x in w], scale=0.5)
 
-    quant(half(T.q0, 0), half(T.p0, 0), T.xs[:, 0:512], ["xs0"], ["q00"])
     scores(0, 0, 0, ["q00"])
-    quant(T.qx[:], T.px[:], T.xc[:], xall, ["qx"])
-    act(T.src[:], T.ty[:].indirect(T.so[:]), ["ty", "so"], ["src"])
-    flags(0, 0, 0)
+    def first(b):
+        unpack(b, 4 + b, T.q0[:], T.p0[:], 256, ["q00", "q01"])
+        keep(b, 4 + b, T.fh, 0, 256, ["f%d0", "f%d1"])
+
+    flags(0, 0, 0, 0, [2])
     quant(half(T.q0, 1), half(T.p0, 1), T.xs[:, 512:1024], ["xs1"], ["q01"])
     scores(0, 1, 1, ["q01"])
-    unpack(T.q0[:], T.p0[:], 256, ["q00", "q01"])
-    keep(T.fh, 0, 256, ["f%d0", "f%d1"])
+    flags(0, 0, 0, 0, [0, 1])
+    first(0)
     packed(0)
-    count(0, 0, True, False, "ab0")
-    tr(T.tf[:, 0:128], T.ft[:, 0:128], ["ft00"], ["tf"])
-    flags(0, 1, 1)
+    count(0, True, False, "ab0")
+    first(1)
+    flags(0, 1, 1, 2)
     packed(1)
-    count(1, 32, False, True, "ab0")
+    count(1, False, True, "ab0")
     quant(T.qm[:], T.pm[:], T.ms[:], ["ms"], ["qm"])
-    unpack(T.qm[:], T.pm[:], 256, ["qm"])
-    keep(T.mh, 0, 256, ["m%d"])
-    tt(T.ab[:], bank[2][:, 0:32], T.jt[:, 0:32], A.add, ["b2", "jt0", "jt"], ["ab"])
+    first(2), first(3)
+    tr(T.tf[:, 0:64], T.ft[:, 0:64], ["ft0"], ["tf"])
+    scan(T.sc[:, 0:32], T.jt[:, 0:32], bank[2][:, 0:32], ["b2", "jt0"], ["sc"])
+    ts(T.go[:, 0:6:2], T.rn[:, 0:3], T.tf[:, 0:1], 255.0, A.add, A.min, ["rn", "tf"], ["go"])
+    mbank = (3, 0, 1, 2)
+    for b in range(4):
+        unpack(b, mbank[b], T.qm[:], T.pm[:], 256, ["qm"])
+    for b in range(2):
+        keep(b, mbank[b], T.mh, 0, 256, ["m%d"])
 
     for k in range(1, 4):
         q, p, iw = T["q%d" % k], T["p%d" % k], T["iw%d" % k]
+        ts(T.po[:], T.sc[:, 1:32:2] if k == 1 else T.sc[:, 2:48:3], col(3), col(3), A.add, A.add, ["sc", "cf"], ["po"])
         if k == 1:
-            cp(T.go[:, 0:4:2], T.tf[:, 0:64:32], ["tf"], ["go0"], "go")
-        tt(T.mn[:], T.ab[:, 0:16], T.ab[:, 16:32], A.min, ["ab"], ["mn"])
+            cp(T.srt[:].indirect(T.po[:]), T.s0[:], ["po", "s0a", "s0b"], ["srt"])
+        else:
+            cp(T.srt[:].indirect(T.po[:]), T.src[:], ["po", "src"], ["srt"])
+        side = lambda j: T.tt[:, 256 * j:256 * j + 256]
+        both = lambda j: ["tt%d" % (2 * j), "tt%d" % (2 * j + 1), "go"]
+
+        def turn(s):
+            a = (0, 32, 1, 33)[s]
+            tr(half(T.tt, s), T.srt[:, a:a + 255:2], ["srt"], ["tt%d" % s], "tt%d%d" % (k, s // 2))
+
+        turn(0), turn(1), turn(2)
+        ts(T.lh[:, 0:16], side(0).indirect(T.go[:, 0:1]), 0.0, None, A.add, None, both(0), ["lh0"])
+        turn(3)
+        ts(T.gn[:, 0:16], side(0).indirect(T.go[:, 4:5]), 16.0, None, A.mult, None, both(0), ["gn0"])
+        tt(T.gn[:, 16:32], side(1).indirect(T.go[:, 2:3]), T.gn[:, 0:16], A.add, both(1) + ["gn0"], ["gn1"])
+        ts(T.lh[:, 16:32], side(1).indirect(T.go[:, 0:1]), 0.0, None, A.add, None, both(1), ["lh1"])
+        cp(T.no[:], T.gn[:, 16:24], ["gn1"], ["no"])
         if k == 1:
-            cp(T.go[:, 4:6], T.tf[:, 64:128:32], ["tf"], ["go"], "go")
-        ts(T.po[:], T.mn[:], col(3), 256.0, A.add, A.add, ["mn", "cf3"], ["po"])
-        cp(T.srt[:].indirect(T.po[:]), T.src[:], ["po", "src"], ["srt"])
-        for j in range(2):
-            for s in (2 * j, 2 * j + 1):
-                a = (0, 32, 1, 33)[s]
-                tr(half(T.tt, s), T.srt[:, a:a + 255:2], ["srt"], ["tt%d" % s], "tt%d%d" % (k, j))
-            ts(T.lh[:, 16 * j:16 * j + 16], T.tt[:, 256 * j:256 * j + 256].indirect(T.go[:, 0:1]), 0.0, None, A.add, None,
-               ["tt%d" % (2 * j), "tt%d" % (2 * j + 1), "go"], ["lh%d" % j])
-        tts = ["tt%d" % s for s in range(4)]
-        cp(T.gn[:, 0:16], T.tt[:].indirect(T.go[:, 2:3]), tts + ["go"], ["gn0"])
+            ts(T.go[:, 6:8], T.jr[:, 80:82], T.tf[:, 32:33], None, A.add, None, ["tf"], ["gp"])
         for b in range(4):
             act(half(T.lf, b), T.fh[:, 256 * b:256 * b + 256].indirect(T.lh[:, 0:8]),
                 ["lh0", "f%d0" % b, "f%d1" % b], ["lf%d" % b])
-        act(iw[:, 32:64], T.tt[:].indirect(T.go[:, 4:6]), tts + ["go"], ["iw%d1" % k])
-        send(k, iw[:, 0:32], iw[:, 32:64], "ri%d" % k, ["iw%d1" % k])
+            if b == 1:
+                act(iw[:, 32:64], T.tt[:].indirect(T.go[:, 6:8]), both(0) + both(1) + ["gp"], ["iw%d1" % k])
+                send(k, iw[:, 0:32], iw[:, 32:64], "ri%d" % k, ["iw%d1" % k])
+        if k == 1:
+            for b in range(2, 4):
+                keep(b, mbank[b], T.mh, 0, 256, ["m%d"])
 
         def larger(b):
             tt(half(T.ph, b), T.fh[:, 256 * b:256 * b + 256].indirect(T.lh[:, 16:24]), half(T.lf, b), A.max,
@@ -339,20 +347,26 @@ def rank_program(g, core, T, topo):
             tt(T.zt[:, b:512:4], T.mh[:, 256 * b:256 * b + 256].indirect(T.no[:]), half(T.ph, b), A.add,
                ["no", "m%d" % b, "ph%d" % b], ["zt%d" % b], "zt%d" % k)
 
-        larger(0)
-        tt(T.gn[:, 16:24], T.gn[:, 0:8], T.gn[:, 8:16], A.add, ["gn0"], ["gn1"])
-        larger(1)
-        cp(T.no[:], T.gn[:, 16:24], ["gn1"], ["no"])
-        larger(2), middle(0), larger(3), middle(1), middle(2), middle(3)
+        larger(0), larger(1), middle(0), larger(2), middle(1), larger(3), middle(2), middle(3)
         quant(T.qz[:], T.pz[:], T.zt[:], ["zt%d" % b for b in range(4)], ["qz"])
         for b in range(4):
             mm(bank[4 + b][:, 0:128], half(T.wq, b), half(T.wp, b), T.qz[:], T.pz[:], ["wq", "wp", "qz"], ["b%d" % (4 + b)])
-        for b in range(4):
+        if k == 1:
+            ts(col(4), col(0), 0.0625, None, A.mult, None, ["cf"], ["cg0"], "cg")
+            ts(col(5), col(0), 0.125, None, A.mult, None, ["cf"], ["cg1"], "cg")
+            ts(col(6), col(0), 0.0625, col(3), A.mult, A.add, ["cf"], ["cg2"], "cg")
+            fill(T.own[:, 0:48:3], LOW, ["own0"])
+
+        def add(b):
             tt(half(T.v32, b), bank[4 + b][:, 0:128], half(T.p32, b), A.add, ["b%d" % (4 + b), "p32%d" % b], ["v32%d" % b])
-            if b < 2:
-                act(T.vt[:, b:512:4], half(T.v32, b), ["v32%d" % b], ["vt%d" % b], scale=0.03125, grp="vt%d" % k)
-        for b in (2, 3):
-            ts(T.vt[:, b:512:4], half(T.v32, b), 0.03125, None, A.mult, None, ["v32%d" % b], ["vt%d" % b], "vu%d" % k)
+
+        def small(b):
+            ts(T.vt[:, b:512:4], half(T.v32, b), 0.03125, None, A.mult, None, ["v32%d" % b], ["vt%d" % b])
+
+        for b in range(2):
+            add(b)
+            act(T.vt[:, b:512:4], half(T.v32, b), ["v32%d" % b], ["vt%d" % b], scale=0.03125, grp="vt%d" % k)
+        add(2), add(3), small(2), small(3)
         quant(half(q, 1), half(p, 1), T.vt[:], ["vt%d" % b for b in range(4)], ["q%d1" % k])
         send(k, raw(half(q, 0)), raw(half(q, 1)), "rq%d" % k, ["q%d1" % k])
         send(k, half(p, 0), half(p, 1), "rp%d" % k, ["q%d1" % k])
@@ -360,54 +374,71 @@ def rank_program(g, core, T, topo):
         arrive(k, "rq%d" % k, ["aq%d" % k])
         arrive(k, "rp%d" % k, ["ap%d" % k])
 
-        def relist(last):
+        def relist():
             for h in range(2):
-                c = 256 * h
-                cp(T.yw[:, c + 1:c + 256:16], iw[:, 32 * h:32 * h + 16], ["iw%d%d" % (k, h)], ["ya%d" % h], "y%d" % k)
-                ts(T.yw[:, c + 2:c + 256:16], iw[:, 32 * h + 16:32 * h + 32], 0.0625 if last else 1.0, None, A.mult, None,
-                   ["iw%d%d" % (k, h)], ["yb%d" % h], "y%d" % k)
-            rows(["ya0", "ya1", "yb0", "yb1"])
+                for t in range(2):
+                    cp(T.yw[:, 256 * h + 1 + t:256 * h + 256:16], iw[:, 32 * h + 16 * t:32 * h + 16 * t + 16],
+                       ["iw%d%d" % (k, h), "yw"], ["ya%d%d" % (h, t)], "y%d" % k)
+            tr(T.ty[:], T.yw[:], ["ya00", "yw", "yc0"], ["ty"])
 
         if k < 3:
             cs, cr = T["cs%d" % k], T["cr%d" % k]
             scores(k, 1, 0, ["q%d1" % k])
-            unpack(half(q, 1), half(p, 1), 128, ["q%d1" % k])
-            flags(k, 0, 0)
+            if k == 1:
+                for t, o in enumerate((A.is_le, A.not_equal)):
+                    ts(half(T.kk, 4 + t), T.rn[:], col(4), FAR, o, A.mult, ["rn", "cg0"], ["kk%d" % (4 + t)], "kk2")
+                ts(T.so[:], T.jr[:, 0:16], 2.0, col(6), A.mult, A.add, ["jr0", "cg2"], ["so"])
+                act(T.jt[:, 32:48], T.jr[:, 16:32], ["jr1", "cg1"], ["jt2"], bias=col(5))
+                act(T.yw[:], T.eb[:, 0:512], ["eb"], ["yw"])
+                act(T.yw[:, 0:512:32], T.jr[:, 0:16], ["jr0", "cg0", "yw"], ["yc0"], bias=col(4), grp="yc")
+                act(T.yw[:, 16:512:32], T.jr[:, 0:16], ["jr0", "cg0", "yw"], ["yc1"], bias=col(4), grp="yc")
+            for b in range(2):
+                unpack(b, 4 + b, half(q, 1), half(p, 1), 128, ["q%d1" % k])
+            flags(k, 0, 0, 4)
             packed(0)
-            count(0, 0, True, True, None)
-            cp(cs[:], bank[2][:, 96:128], ["b2"], ["cs%d" % k])
+            count(0, True, True, None)
+            for b in range(2, 4):
+                unpack(b, 4 + b, half(q, 1), half(p, 1), 128, ["q%d1" % k])
+            if k == 1:
+                tr(T.tf[:, 64:128], T.ft[:, 64:128], ["ft4"], ["tg"])
+                quant(T.qv[:], T.pv[:], T.vs[:], ["vs"], ["qv"])
+            cp(cs[:], bank[2][:, 80:128], ["b2"], ["cs%d" % k])
             send(k, cr[:], cs[:], "rc%d" % k, ["cs%d" % k])
             arrive(k, "rc%d" % k, ["cr%d" % k])
-            keep(T.fh, 128, 128, ["f%d1"])
-            if k == 1:
-                ts(T.jt[:, 48:64], T.jr[:, 16:32], col(2), None, A.add, None, ["jr1", "cf2", "jt"], ["jt1"])
-                tr(T.tf[:, 128:192], T.ft[:, 128:192], ["ft4"], ["tg"])
-            tt(T.own[:], bank[2][:, 64:96], T.jt[:, 32:64], A.add, ["b2", "jt1", "jt"], ["own"])
-            relist(False)
+            for b in range(4):
+                keep(b, 4 + b, T.fh, 128, 128, ["f%d1"])
+            tt(T.hi[:], bank[2][:, 32:80:3], T.jt[:, 32:48], A.add, ["b2", "jt2"], ["hi"])
+            cp(T.own[:, 2:48:3], bank[2][:, 33:80:3], ["b2"], ["own2"])
+            relist()
+            tt(T.own[:, 1:48:3], T.hi[:], T.own[:, 2:48:3], A.subtract, ["hi", "own2"], ["own1"])
             act(T.src[:], T.ty[:].indirect(T.so[:]), ["ty", "so"], ["src"])
             if k == 1:
-                quant(T.qv[:], T.pv[:], T.vs[:], ["vs"], ["qv"])
-                ts(T.fo[:], T.jr[:, 0:16], 0.5, T.tf[:, 128:129], A.mult, A.add, ["jr0", "tg"], ["fo"])
-                ts(T.lo[:], T.jr[:, 32:48], T.tf[:, 160:161], None, A.add, None, ["jr2", "tg"], ["lo"])
-            unpack(half(q, 0), half(p, 0), 128, ["aq%d" % k, "ap%d" % k])
-            keep(T.fh, 0, 128, ["f%d0"])
-            tt(T.ab[:], T.own[:], cr[:], A.add, ["own", "cr%d" % k], ["ab"])
+                ts(T.fo[:], T.jr[:, 0:16], 0.5, T.tf[:, 64:65], A.mult, A.add, ["jr0", "tg"], ["fo"])
+                ts(T.lo[:], T.jr[:, 32:48], T.tf[:, 96:97], None, A.add, None, ["jr2", "tg"], ["lo"])
+            for b in range(4):
+                unpack(b, 4 + b, half(q, 0), half(p, 0), 128, ["aq%d" % k, "ap%d" % k])
+                keep(b, 4 + b, T.fh, 0, 128, ["f%d0"])
+            scan(T.sc[:], T.own[:], cr[:], ["own0", "own1", "own2", "cr%d" % k], ["sc"])
         else:
             mm(bank[0][:, 0:128], T.qv[:], T.pv[:], half(q, 1), half(p, 1), ["qv", "q31"], ["b0"])
-            relist(True)
+            relist()
             cp(T.yo[:, 1:256:2], bank[0][:, 0:128], ["b0"], ["yo1"])
             act(T.lro[:], T.ty[:].indirect(T.lo[:]), ["ty", "lo"], ["lro"])
             dma("y", T.lr[:, 0:256], T.lro[1:128:16, :], ["lro"], ["o0"], "out0")
             dma("y", T.lr[:, 256:512], T.lro[2:128:16, :], ["lro"], ["o1"], "out0")
             mm(bank[1][:, 0:128], T.qv[:], T.pv[:], half(q, 0), half(p, 0), ["qv", "aq3", "ap3"], ["b1"])
-            for h in range(2):
+            act(T.pf[:], p[:].indirect(T.fo[:]), ["ap3", "q31", "fo"], ["pf"])
+
+            def codes(h):
                 cp(words(half(T.qf, h)), words(q[:]).indirect(T.fo[:, 8 * h:8 * h + 8]), ["aq3", "q31", "fo"], ["qf%d" % h])
-                act(half(T.pf, h), p[:].indirect(T.fo[:, 8 * h:8 * h + 8]), ["ap3", "q31", "fo"], ["pf%d" % h], grp="pf")
                 dma("y", T.oc[:, 512 * h:512 * h + 512], raw(half(T.qf, h)), ["qf%d" % h], ["o2%d" % h], "out1")
+
+            codes(0)
             cp(T.yo[:, 0:256:2], bank[1][:, 0:128], ["b1"], ["yo0"])
             dma("y", T.y[:], T.yo[:], ["yo0", "yo1"], ["o3"], "out1")
+            codes(1)
             for j in range(4):
-                dma("s", T.osc[4 * j:4 * j + 4, :], T.pf[32 * j:32 * j + 4, :], ["pf0", "pf1"], ["o4%d" % j], "out2")
+                dma("s", T.osc[4 * j:4 * j + 4, :], T.pf[32 * j:32 * j + 4, :], ["pf"], ["o4%d" % j], "out2")
     op("y", None, ["o0", "o3", "o40"], [])
     emit(ops, queues, T)
     g.wait_ge(T.sem.sent, sent[0])

@@ -3,7 +3,8 @@ from concourse.mybir import dt, AluOpType, ActivationFunctionType
 BF, F32, I32, U16, U8, MX = "bfloat16", "float32", "int32", "uint16", "uint8", "float8_e4m3fn_x4"
 DIST = [1, 2, 4]
 FAR = float(2 ** 80)
-LOW = -1024.0
+TINY = float(2.0 ** -110)
+LOW = -4096.0
 
 SCRATCH = {
     "xs": ("sbuf", [128, 1024], BF), "us": ("sbuf", [128, 512], BF), "ms": ("sbuf", [128, 1024], BF),
@@ -14,19 +15,20 @@ SCRATCH = {
     "qv": ("sbuf", [128, 128], MX), "pv": ("sbuf", [128, 128], U8),
     "qm": ("sbuf", [128, 256], MX), "pm": ("sbuf", [128, 256], U8),
     "ip": ("sbuf", [128, 2], I32), "bi": ("sbuf", [128, 4], I32), "cf": ("sbuf", [128, 8], F32),
-    "rn": ("sbuf", [128, 128], BF), "dg": ("sbuf", [128, 128], BF), "jr": ("sbuf", [128, 96], F32),
-    "tq": ("sbuf", [128, 16], BF),
+    "rn": ("sbuf", [128, 128], BF), "dg": ("sbuf", [128, 128], BF), "jr": ("sbuf", [128, 128], F32),
+    "tq": ("sbuf", [128, 32], BF),
     "eb": ("sbuf", [128, 516], BF), "qe": ("sbuf", [128, 512], MX), "pe": ("sbuf", [128, 512], U8),
     "kk": ("sbuf", [128, 768], BF),
-    "xc": ("sbuf", [128, 512], BF), "qx": ("sbuf", [128, 128], MX), "px": ("sbuf", [128, 128], U8),
-    "jt": ("sbuf", [128, 48], F32), "ft": ("sbuf", [128, 128], F32), "tf": ("sbuf", [128, 128], F32),
+    "xc": ("sbuf", [128, 512], BF), "qx": ("sbuf", [128, 256], MX), "px": ("sbuf", [128, 256], U8),
+    "jt": ("sbuf", [128, 64], F32), "ft": ("sbuf", [128, 288], F32), "tf": ("sbuf", [128, 288], F32),
     "uo": ("sbuf", [128, 8], U16), "so": ("sbuf", [128, 16], U16), "go": ("sbuf", [128, 8], U16),
     "fo": ("sbuf", [128, 16], U16), "lo": ("sbuf", [128, 16], U16),
-    "wf": ("sbuf", [128, 1024], BF), "qw": ("sbuf", [128, 256], MX), "pw": ("sbuf", [128, 256], U8),
-    "hi": ("sbuf", [128, 16], F32), "own": ("sbuf", [128, 48], F32), "sc": ("sbuf", [128, 48], F32),
+    "wf": ("sbuf", [128, 512], BF), "qw": ("sbuf", [128, 128], MX), "pw": ("sbuf", [128, 128], U8),
+    "sg": ("sbuf", [128, 256], BF), "sm": ("sbuf", [128, 1], F32), "cs": ("sbuf", [128, 128], BF),
+    "hi": ("sbuf", [128, 16], F32), "own": ("sbuf", [128, 64], F32), "sc": ("sbuf", [128, 64], F32),
     "po": ("sbuf", [128, 16], U16), "yw": ("sbuf", [128, 512], BF), "ty": ("sbuf", [128, 512], BF),
-    "src": ("sbuf", [128, 256], BF), "srt": ("sbuf", [128, 288], BF), "tt": ("sbuf", [128, 512], BF),
-    "gn": ("sbuf", [128, 32], F32), "lh": ("sbuf", [128, 32], U16), "no": ("sbuf", [128, 8], U16),
+    "src": ("sbuf", [128, 256], BF), "srt": ("sbuf", [128, 288], BF), "tt": ("sbuf", [128, 528], BF),
+    "gn": ("sbuf", [128, 16], BF), "lh": ("sbuf", [128, 48], U16),
     "fh": ("sbuf", [128, 1024], BF), "mh": ("sbuf", [128, 1024], BF), "lf": ("sbuf", [128, 512], BF),
     "ph": ("sbuf", [128, 512], BF), "p32": ("sbuf", [128, 512], BF), "zt": ("sbuf", [128, 512], BF),
     "qz": ("sbuf", [128, 128], MX), "pz": ("sbuf", [128, 128], U8),
@@ -40,12 +42,11 @@ for _k in range(4):
 for _k in range(1, 4):
     SCRATCH["iw%d" % _k] = ("sbuf", [128, 64], BF)
 for _k in range(1, 3):
-    SCRATCH["cs%d" % _k] = ("sbuf", [128, 48], BF)
-    SCRATCH["cr%d" % _k] = ("sbuf", [128, 48], BF)
+    SCRATCH["cr%d" % _k] = ("sbuf", [128, 64], BF)
 for _k in range(8):
     SCRATCH["b%d" % _k] = ("psum", [128, 512], F32)
 
-POOL = {"v": 56, "s": 30, "t": 20, "g": 12, "d": 14}
+POOL = {"v": 56, "s": 30, "t": 20, "g": 14, "d": 14}
 ARRIVE = ["ri1", "ri2", "ri3", "rq1", "rq2", "rq3", "rp1", "rp2", "rp3", "rc1", "rc2"]
 SEMAPHORES = ["%s%d" % (q, i) for q in POOL for i in range(POOL[q])] + ARRIVE + ["sent"]
 
@@ -156,8 +157,8 @@ def rank_program(g, core, T, topo):
         else:
             op("s", lambda: sca.activation(out, in_, ACT.Copy), r, w, grp)
 
-    def mm(out, lq, lp, rq, rp, r, w, start=True, stop=True, grp=None):
-        op("t", lambda: ten.matmul_mx(out, lq, lp, rq, rp, start, stop), r, w, grp)
+    def mm(out, lq, lp, rq, rp, r, w):
+        op("t", lambda: ten.matmul_mx(out, lq, lp, rq, rp, True, True), r, w)
 
     def iota(out, pattern, base, cm, w, grp=None, whole=False):
         if whole:
@@ -180,6 +181,7 @@ def rank_program(g, core, T, topo):
 
     bank = [T["b%d" % k] for k in range(8)]
     col = lambda c: T.cf[:, c:c + 1]
+    turned = lambda k: T.tf[:, 32 * k:32 * k + 1]
     words = lambda v: v.bitcast(dt.uint32)
     raw = lambda v: v.bitcast(dt.uint8)
 
@@ -189,88 +191,88 @@ def rank_program(g, core, T, topo):
     dma("y", T.us[:], T.u[:], [], ["us"])
     dma("y", T.xs[:, 0:512], T.x[:, 0:512], [], ["xs0"])
     dma("y", T.xs[:, 512:1024], T.x[:, 512:1024], [], ["xs1"])
-    dma("y", T.ms[:], T.mid[:], [], ["ms"])
+    dma("y", T.ms[:, 0:512], T.mid[:, 0:512], [], ["ms0"])
+    dma("y", T.ms[:, 512:1024], T.mid[:, 512:1024], [], ["ms1"])
 
+    x1 = lambda kind, t: T.xc[:, 4 * kind + t:128:8]
+    x2 = lambda kind, t, a, b: T.xc[:, 128 + 8 * a + 4 * kind + t:128 + 8 * b:8]
     iota(T.ip[:], [[2048, 2]], 0, 16, ["ip"], whole=True)
     iota(T.dg[:], [[1, 128]], 0, -1, ["dg"])
-    iota(T.jr[:, 48:80], [[0, 4], [1, 8]], 0, 0, ["jr3"])
     iota(T.jr[:, 0:16], [[16, 16]], 0, 0, ["jr0"])
     iota(T.rn[:], [[0, 8], [1, 16]], 0, 0, ["rn"])
+    iota(T.xc[:, 0:128:2], [[0, 16], [4, 2], [0, 2]], -2, 0, ["xa"])
     iota(T.s0[:], [[1, 16], [16, 16]], 0, 0, ["s0"], whole=True)
+    iota(T.jr[:, 96:112], [[1, 16]], 128, 0, ["jr5"])
     dma("y", T.s0[1:128:16, :], T.li[:], ["s0"], ["s0a"], "lists")
     dma("y", T.s0[2:128:16, :], T.ri[:], ["s0"], ["s0b"], "lists")
     dma("y", T.wp[:], T.ws[:], [], ["wp"], "layer")
     dma("y", raw(T.wq[:]), T.wc[:], [], ["wq"], "layer")
     dma("y", T.vs[:], T.v[:], [], ["vs"])
-    iota(T.ft[:, 0:32], [[16, 2], [32, 8], [128, 2]], 0, 0, ["ft0"], "ft")
     for h in range(2):
+        iota(T.ft[:, 16 * h:16 + 16 * h], [[0, 2], [32, 4], [128, 2]], 16 * h, 0, ["ft0%d" % h], "ft")
         iota(T.ft[:, 32 + 16 * h:48 + 16 * h], [[32, 4], [128, 2], [0, 2]], 16 * h, 0, ["ft1%d" % h], "ft")
-    iota(T.jr[:, 80:82], [[257, 2]], 1, 0, ["jr4"], "ft")
-    iota(T.ft[:, 64:96], [[0, 2], [1, 8], [128, 2]], 0, 0, ["ft4"], "fu")
-    iota(T.ft[:, 96:128], [[16, 2], [1, 8], [256, 2]], 0, 0, ["ft5"], "fu")
-    iota(T.jr[:, 16:32], [[1, 2], [32, 8]], 0, 0, ["jr1"], "fu")
-    iota(T.jr[:, 32:48], [[32, 8], [8, 2]], 0, 0, ["jr2"], "fu")
+        iota(T.ft[:, 64 + 16 * h:72 + 16 * h], [[32, 4], [128, 2]], 16 * h, 0, ["ft2%d" % h], "ft")
+        iota(T.ft[:, 72 + 16 * h:80 + 16 * h], [[2, 4], [8, 2]], 256 + h, 0, ["ft3%d" % h], "ft")
+    iota(T.jr[:, 80:82], [[257, 2]], 1, 0, ["jr4"])
+    for k, pattern in enumerate(([[0, 4], [16, 8]], [[0, 2], [1, 2], [0, 8]], [[0, 2], [1, 16]],
+                                 [[16, 2], [32, 8], [8, 2]], [[0, 2], [1, 8], [128, 2]], [[16, 2], [1, 8], [256, 2]])):
+        iota(T.ft[:, 96 + 32 * k:128 + 32 * k], pattern, 0, 0, ["fu%d" % k], "fu%d" % (k // 3))
+    iota(T.jr[:, 48:72], [[0, 3], [16, 8]], 0, 0, ["jr3"], "fv")
+    iota(T.jr[:, 16:32], [[1, 2], [2, 8]], 128, 0, ["jr1"], "fv")
+    iota(T.jr[:, 32:48], [[32, 8], [8, 2]], 0, 0, ["jr2"], "fv")
+    iota(T.jr[:, 112:128], [[256, 2], [1, 8]], 0, 0, ["jr6"], "fv")
 
-    x1 = lambda kind, t: T.xc[:, 4 * kind + t:128:8]
-    x2 = lambda kind, t, a=0, b=32: T.xc[:, 128 + 12 * a + 4 * kind + t:128 + 12 * b:12]
+    def unit(b):
+        quant(half(T.qe, b), half(T.pe, b), T.eb[:, 3 - b:515 - b], ["eb"], ["qe%d" % b])
+
+    def thresholds(c, block, r):
+        for t, o in enumerate((A.is_le, A.not_equal)):
+            ts(half(T.kk, c + t), T.rn[:], block, FAR, o, A.mult, ["rn"] + r, ["kk%d" % (c + t)], "kk%d" % c)
+
     fill(T.eb[:], 0.0, ["eb"])
-    fill(T.xc[:], 0.0, ["xc"])
+    fill(T.xc[:, 128:512], 0.0, ["xc"])
     ts(T.bi[:, 0:1], T.ip[:, 0:1], 255, None, A.bitwise_and, None, ["ip"], ["bi0"], "bi")
     ts(T.bi[:, 1:3], T.ip[:], 8, None, A.arith_shift_right, None, ["ip"], ["bi1"], "bi")
-    ts(T.bi[:, 3:4], T.ip[:, 0:1], 4, 16, A.arith_shift_right, A.bitwise_and, ["ip"], ["bi2"], "bi")
+    ts(T.bi[:, 3:4], T.ip[:, 0:1], 3, 32, A.arith_shift_right, A.bitwise_and, ["ip"], ["bi2"], "bi")
     ts(T.eb[:, 3:515:4], T.dg[:], 0.0, None, A.is_equal, None, ["dg", "eb"], ["eb"])
     cp(T.cf[:, 0:4], T.bi[:], ["bi0"], ["cf"])
-    quant(half(T.qe, 0), half(T.pe, 0), T.eb[:, 3:515], ["eb"], ["qe0"], "qe")
-    ts(x2(1, 2), T.jr[:, 48:80], col(1), None, A.is_gt, None, ["jr3", "cf", "xc"], ["xu"], "xa")
-    ts(x2(1, 0), T.jr[:, 48:80], col(1), None, A.is_equal, None, ["jr3", "cf", "xc"], ["xe"], "xa")
-    for b in range(1, 4):
-        quant(half(T.qe, b), half(T.pe, b), T.eb[:, 3 - b:515 - b], ["eb"], ["qe%d" % b], "qe")
-    zero = T.xc[:, 3:128:8]
-    act(x1(1, 0), zero, ["xc"], ["xb0"], bias=1.0, grp="xb")
-    act(x1(0, 2), zero, ["xc"], ["xb1"], bias=1.0, grp="xb")
-    act(x1(0, 0), zero, ["xc"], ["xb2"], bias=-1.0, grp="xb")
-    act(x2(0, 2), x2(1, 2), ["xu"], ["xb3"], scale=-1.0, bias=1.0, grp="xb")
-    act(x2(0, 0), x2(1, 0), ["xe"], ["xb4"], scale=-1.0, grp="xb")
-    act(x2(0, 1, 8, 24), x2(1, 0, 8, 24), ["xe"], ["xb5"], scale=-256.0, grp="xb")
-    act(x2(0, 1, 24, 32), x2(1, 0, 24, 32), ["xe"], ["xb6"], scale=-1.0, grp="xb")
-    act(x2(1, 1, 24, 32), x2(1, 0, 24, 32), ["xe"], ["xb7"], grp="xb")
-    act(T.wf[:, 3:1024:4], T.eb[:, 0:256], ["eb"], ["wz"])
-    act(T.srt[:], T.eb[:, 0:288], ["eb"], ["srt"])
-    ts(x1(1, 1), T.jr[:, 0:16], col(0), None, A.is_gt, None, ["jr0", "cf", "xc"], ["xt"], "xd")
-    ts(T.tq[:], T.jr[:, 0:16], col(0), -256.0, A.is_equal, A.mult, ["jr0", "cf"], ["tq"], "xd")
     cp(T.uo[:], T.jr[:, 0:8], ["jr0"], ["uo"])
-    for h in range(2):
-        for t, o in enumerate((A.is_le, A.not_equal)):
-            ts(half(T.kk, 2 * h + t), T.rn[:], col(1 + h), FAR, o, A.mult, ["rn", "cf"], ["kk%d" % (2 * h + t)], "kk%d" % h)
-        if h == 0:
-            tt(x1(0, 1), T.tq[:], x1(1, 1), A.subtract, ["tq", "xt"], ["xv"])
-    act(T.jt[:, 0:32:2], zero, ["xc"], ["jt0"], bias=LOW, grp="jt")
-    act(T.jt[:, 1:32:2], T.rn[:, 0:16], ["rn", "cf"], ["jt1"], bias=col(0), grp="jt")
+    unit(0)
+    ts(x1(1, 1), T.jr[:, 0:16], col(0), 2.0, A.is_gt, A.mult, ["jr0", "cf"], ["xt"], "xd")
+    ts(T.tq[:, 0:16], T.jr[:, 0:16], col(0), -512.0, A.is_equal, A.mult, ["jr0", "cf"], ["tq"], "xd")
+    unit(1)
+    tt(x1(0, 1), T.tq[:, 0:16], x1(1, 1), A.subtract, ["tq", "xt"], ["xv"])
+    act(x1(1, 3), x1(1, 1), ["xt"], ["xb0"], grp="xb")
+    act(x1(0, 3), x1(0, 1), ["xv"], ["xb1"], grp="xb")
 
     quant(T.qu[:], T.pu[:], T.us[:], ["us"], ["qu"])
-    quant(T.qx[:], T.px[:], T.xc[:], ["xc", "xu", "xb0", "xt", "xv"], ["qx"])
+    thresholds(0, col(1), ["cf"])
     cp(words(T.qg[:]), words(T.qu[:]).indirect(T.uo[:, 0:8]), ["qu", "uo"], ["qg"])
     act(T.pg[:], T.pu[:].indirect(T.uo[:, 0:8]), ["qu", "uo"], ["pg"])
+    act(T.srt[:], T.eb[:, 0:288], ["eb"], ["srt"])
+    act(T.jt[:, 0:32:2], T.rn[:, 0:16], ["rn"], ["jt0"], scale=0.0, bias=LOW)
+    act(T.jt[:, 32:48], T.jr[:, 96:112], ["jr5", "cf"], ["jt2"], bias=col(0))
+    act(T.yw[:], T.eb[:, 0:512], ["eb"], ["yw"])
+    unit(2)
     quant(half(T.q0, 0), half(T.p0, 0), T.xs[:, 0:512], ["xs0"], ["q00"])
 
     def scores(k, h, bk, r):
         mm(bank[bk][:, 0:128], half(T["q%d" % k], h), half(T["p%d" % k], h), T.qg[:], T.pg[:],
            r + ["qg", "pg"], ["b%d" % bk])
 
-    def flags(k, i, bk, kk, slots=(2, 0, 1)):
-        grp = "fl%d%d" % (k, i)
-        for t in slots:
-            w = T.wf[:, 512 * i + t:512 * i + 512:4]
-            if t == 2:
-                ts(w, bank[bk][:, 0:128], 0.0, None, A.is_gt, None, ["b%d" % bk], ["w%d2" % i], grp)
-            else:
-                tt(w, bank[bk][:, 0:128], half(T.kk, kk + t), A.is_gt, ["b%d" % bk, "kk%d" % (kk + t)], ["w%d%d" % (i, t)], grp)
+    def total(bk, q, p, n, r):
+        mm(bank[bk][:, 0:n], T.qg[:], T.pg[:], q, p, r + ["qg", "pg"], ["b%d" % bk])
+        op("s", lambda: sca.activation(T.sg[:, 0:n], bank[bk][:, 0:n], ACT.Sign, bias=-TINY, accum_out=T.sm[:]),
+           ["b%d" % bk], ["sm"])
 
-    def packed(i):
-        quant(half(T.qw, i), half(T.pw, i), T.wf[:, 512 * i:512 * i + 512], ["w%d%d" % (i, t) for t in range(3)] + ["wz"], ["qw%d" % i])
+    def flags(grp, slot, bk, kk):
+        for t in range(2):
+            tt(T.wf[:, slot + t:512:4], bank[bk][:, 0:128], half(T.kk, kk + t), A.is_gt,
+               ["b%d" % bk, "kk%d" % (kk + t)], ["w%d" % (slot + t)], grp)
 
-    def count(i, start, stop, grp):
-        mm(bank[2][:, 0:128], half(T.qw, i), half(T.pw, i), T.qx[:], T.px[:], ["qw%d" % i, "qx"], ["b2"], start, stop, grp)
+    def count(x):
+        quant(T.qw[:], T.pw[:], T.wf[:], ["w%d" % t for t in range(4)], ["qw"])
+        mm(bank[2][:, 0:128], T.qw[:], T.pw[:], half(T.qx, x), half(T.px, x), ["qw", "qx%d" % x], ["b2"])
 
     def unpack(b, bk, q, p, n, r):
         mm(bank[bk][:, 0:n], half(T.qe, b), half(T.pe, b), q, p, r + ["qe%d" % b], ["b%d" % bk])
@@ -278,39 +280,48 @@ def rank_program(g, core, T, topo):
     def keep(b, bk, dst, c, n, w):
         act(dst[:, 256 * b + c:256 * b + c + n], bank[bk][:, 0:n], ["b%d" % bk], [x % b for x in w], scale=0.5)
 
-    scores(0, 0, 0, ["q00"])
     def first(b):
         unpack(b, 4 + b, T.q0[:], T.p0[:], 256, ["q00", "q01"])
         keep(b, 4 + b, T.fh, 0, 256, ["f%d0", "f%d1"])
 
-    flags(0, 0, 0, 0, [2])
+    scores(0, 0, 0, ["q00"])
+    unit(3)
+    thresholds(2, col(2), ["cf"])
+    quant(half(T.qx, 0), half(T.px, 0), T.xc[:], ["xc", "xa", "xt", "xv", "xb0"], ["qx0"])
     quant(half(T.q0, 1), half(T.p0, 1), T.xs[:, 512:1024], ["xs1"], ["q01"])
     scores(0, 1, 1, ["q01"])
-    flags(0, 0, 0, 0, [0, 1])
+    total(3, T.q0[:], T.p0[:], 256, ["q00", "q01"])
+    act(T.jt[:, 1:32:2], T.jt[:, 32:48], ["jt2", "sm"], ["jt1"], scale=2.0, bias=T.sm[:])
+    flags("fa", 0, 0, 0)
     first(0)
-    packed(0)
-    count(0, True, False, "ab0")
+    flags("fa", 2, 1, 2)
+    count(0)
     first(1)
-    flags(0, 1, 1, 2)
-    packed(1)
-    count(1, False, True, "ab0")
-    quant(T.qm[:], T.pm[:], T.ms[:], ["ms"], ["qm"])
-    first(2), first(3)
-    tr(T.tf[:, 0:64], T.ft[:, 0:64], ["ft0"], ["tf"])
-    scan(T.sc[:, 0:32], T.jt[:, 0:32], bank[2][:, 0:32], ["b2", "jt0"], ["sc"])
-    ts(T.go[:, 0:6:2], T.rn[:, 0:3], T.tf[:, 0:1], 255.0, A.add, A.min, ["rn", "tf"], ["go"])
+    tr(T.tf[:, 0:96], T.ft[:, 0:96], ["ft00"], ["tf"])
+    quant(half(T.qm, 0), half(T.pm, 0), T.ms[:, 0:512], ["ms0"], ["qm0"])
+    cp(T.go[:, 0:4:2], T.tf[:, 0:96:64], ["tf"], ["go"])
+    ts(T.go[:, 4:6], T.jr[:, 80:82], turned(1), None, A.add, None, ["tf", "jr4"], ["gp"])
+    scan(T.sc[:, 0:32], T.jt[:, 0:32], bank[2][:, 0:32], ["b2", "jt0", "jt1"], ["sc"])
+    fill(T.own[:, 1:64:2], LOW, ["own1"])
+    fill(T.cs[:, 0:128:4], LOW, ["cs"])
+    ts(T.po[:], T.sc[:, 1:32:2], 0.5, col(3), A.mult, A.add, ["sc", "cf"], ["po"])
+    quant(half(T.qm, 1), half(T.pm, 1), T.ms[:, 512:1024], ["ms1"], ["qm1"])
+    iota(T.xc[:, 128:256:4], [[0, 16], [4, 2]], -2, 0, ["xc"], "xg")
+    iota(T.xc[:, 256:384:4], [[0, 16], [6, 2]], -4, 0, ["xc"], "xg")
     mbank = (3, 0, 1, 2)
+    first(2), first(3)
     for b in range(4):
-        unpack(b, mbank[b], T.qm[:], T.pm[:], 256, ["qm"])
+        unpack(b, mbank[b], T.qm[:], T.pm[:], 256, ["qm0", "qm1"])
     for b in range(2):
         keep(b, mbank[b], T.mh, 0, 256, ["m%d"])
 
     for k in range(1, 4):
         q, p, iw = T["q%d" % k], T["p%d" % k], T["iw%d" % k]
-        ts(T.po[:], T.sc[:, 1:32:2] if k == 1 else T.sc[:, 2:48:3], col(3), col(3), A.add, A.add, ["sc", "cf"], ["po"])
         if k == 1:
             cp(T.srt[:].indirect(T.po[:]), T.s0[:], ["po", "s0a", "s0b"], ["srt"])
+            tr(T.tf[:, 96:192], T.ft[:, 96:192], ["fu0"], ["tg"])
         else:
+            ts(T.po[:], T.sc[:, 3:64:4], 0.5, col(3), A.mult, A.add, ["sc", "cf"], ["po"])
             cp(T.srt[:].indirect(T.po[:]), T.src[:], ["po", "src"], ["srt"])
         side = lambda j: T.tt[:, 256 * j:256 * j + 256]
         both = lambda j: ["tt%d" % (2 * j), "tt%d" % (2 * j + 1), "go"]
@@ -322,17 +333,19 @@ def rank_program(g, core, T, topo):
         turn(0), turn(1), turn(2)
         ts(T.lh[:, 0:16], side(0).indirect(T.go[:, 0:1]), 0.0, None, A.add, None, both(0), ["lh0"])
         turn(3)
-        ts(T.gn[:, 0:16], side(0).indirect(T.go[:, 4:5]), 16.0, None, A.mult, None, both(0), ["gn0"])
-        tt(T.gn[:, 16:32], side(1).indirect(T.go[:, 2:3]), T.gn[:, 0:16], A.add, both(1) + ["gn0"], ["gn1"])
-        ts(T.lh[:, 16:32], side(1).indirect(T.go[:, 0:1]), 0.0, None, A.add, None, both(1), ["lh1"])
-        cp(T.no[:], T.gn[:, 16:24], ["gn1"], ["no"])
         if k == 1:
-            ts(T.go[:, 6:8], T.jr[:, 80:82], T.tf[:, 32:33], None, A.add, None, ["tf"], ["gp"])
+            ts(T.gn[:], T.tt[:, 2:256:16], 16.0, None, A.mult, None, both(0), ["gn"])
+            ts(T.lh[:, 16:32], side(1).indirect(T.go[:, 0:1]), 0.0, None, A.add, None, both(1), ["lh1"])
+            tt(T.tt[:, 512:528], T.gn[:], T.tt[:, 257:512:16], A.add, both(1) + ["gn"], ["tt4"])
+        else:
+            tt(T.tt[:, 512:528], T.tt[:, 2:256:16], T.tt[:, 257:512:16], A.add, both(0) + both(1), ["tt4"])
+            ts(T.lh[:, 16:32], side(1).indirect(T.go[:, 0:1]), 0.0, None, A.add, None, both(1), ["lh1"])
+        ts(T.lh[:, 32:48], T.tt[:, 256:528].indirect(T.go[:, 2:3]), 0.0, None, A.add, None, both(1) + ["tt4"], ["no"])
         for b in range(4):
             act(half(T.lf, b), T.fh[:, 256 * b:256 * b + 256].indirect(T.lh[:, 0:8]),
                 ["lh0", "f%d0" % b, "f%d1" % b], ["lf%d" % b])
             if b == 1:
-                act(iw[:, 32:64], T.tt[:].indirect(T.go[:, 6:8]), both(0) + both(1) + ["gp"], ["iw%d1" % k])
+                act(iw[:, 32:64], T.tt[:, 0:512].indirect(T.go[:, 4:6]), both(0) + both(1) + ["gp"], ["iw%d1" % k])
                 send(k, iw[:, 0:32], iw[:, 32:64], "ri%d" % k, ["iw%d1" % k])
         if k == 1:
             for b in range(2, 4):
@@ -341,21 +354,29 @@ def rank_program(g, core, T, topo):
         def larger(b):
             tt(half(T.ph, b), T.fh[:, 256 * b:256 * b + 256].indirect(T.lh[:, 16:24]), half(T.lf, b), A.max,
                ["lh1", "lf%d" % b, "f%d0" % b, "f%d1" % b], ["ph%d" % b])
-            act(half(T.p32, b), half(T.ph, b), ["ph%d" % b], ["p32%d" % b], scale=64.0)
+            if b % 2:
+                act(T.p32[:, 128 * b - 128:128 * b + 128], T.ph[:, 128 * b - 128:128 * b + 128], ["ph%d" % (b - 1), "ph%d" % b],
+                    ["p32%d" % (b - 1), "p32%d" % b], scale=64.0)
 
         def middle(b):
-            tt(T.zt[:, b:512:4], T.mh[:, 256 * b:256 * b + 256].indirect(T.no[:]), half(T.ph, b), A.add,
+            tt(T.zt[:, b:512:4], T.mh[:, 256 * b:256 * b + 256].indirect(T.lh[:, 40:48]), half(T.ph, b), A.add,
                ["no", "m%d" % b, "ph%d" % b], ["zt%d" % b], "zt%d" % k)
 
         larger(0), larger(1), middle(0), larger(2), middle(1), larger(3), middle(2), middle(3)
+        if k == 1:
+            tr(T.tf[:, 192:288], T.ft[:, 192:288], ["fu3"], ["th"])
+            act(T.jt[:, 48:64], T.jr[:, 16:32], ["jr1", "cf"], ["jt3"], bias=col(0))
         quant(T.qz[:], T.pz[:], T.zt[:], ["zt%d" % b for b in range(4)], ["qz"])
         for b in range(4):
             mm(bank[4 + b][:, 0:128], half(T.wq, b), half(T.wp, b), T.qz[:], T.pz[:], ["wq", "wp", "qz"], ["b%d" % (4 + b)])
         if k == 1:
-            ts(col(4), col(0), 0.0625, None, A.mult, None, ["cf"], ["cg0"], "cg")
-            ts(col(5), col(0), 0.125, None, A.mult, None, ["cf"], ["cg1"], "cg")
-            ts(col(6), col(0), 0.0625, col(3), A.mult, A.add, ["cf"], ["cg2"], "cg")
-            fill(T.own[:, 0:48:3], LOW, ["own0"])
+            near = T.jr[:, 48:56]
+            ts(col(4), col(1), 2.0, turned(4), A.mult, A.add, ["cf", "tg"], ["cg"])
+            ts(x2(1, 1, 0, 24), T.jr[:, 48:72], turned(3), 2.0, A.is_gt, A.mult, ["tg", "jr3", "xc"], ["xh0"], "xh")
+            ts(T.tq[:, 16:24], near, turned(3), -512.0, A.is_equal, A.mult, ["tg"], ["xh1"], "xh")
+            ts(T.tq[:, 24:32], near, turned(3), 4.0, A.is_gt, A.mult, ["tg"], ["xh2"], "xh")
+            ts(x2(1, 1, 24, 32), near, turned(3), 2.0, A.is_ge, A.mult, ["tg", "xc"], ["xh3"], "xh")
+            ts(x2(0, 1, 24, 32), near, turned(3), -4.0, A.is_ge, A.mult, ["tg", "xc"], ["xh4"], "xh")
 
         def add(b):
             tt(half(T.v32, b), bank[4 + b][:, 0:128], half(T.p32, b), A.add, ["b%d" % (4 + b), "p32%d" % b], ["v32%d" % b])
@@ -363,13 +384,18 @@ def rank_program(g, core, T, topo):
         def small(b):
             ts(T.vt[:, b:512:4], half(T.v32, b), 0.03125, None, A.mult, None, ["v32%d" % b], ["vt%d" % b])
 
-        for b in range(2):
-            add(b)
-            act(T.vt[:, b:512:4], half(T.v32, b), ["v32%d" % b], ["vt%d" % b], scale=0.03125, grp="vt%d" % k)
-        add(2), add(3), small(2), small(3)
+        add(0)
+        act(T.vt[:, 0:512:4], half(T.v32, 0), ["v320"], ["vt0"], scale=0.03125)
+        add(1), add(2), add(3), small(1), small(2), small(3)
+        if k == 1:
+            act(T.yw[:, 0:512:32], T.jr[:, 0:16], ["jr0", "tg", "yw"], ["yc0"], bias=turned(5), grp="yc")
+            act(T.yw[:, 16:512:32], T.jr[:, 0:16], ["jr0", "tg", "yw"], ["yc1"], bias=turned(5), grp="yc")
+            tt(x2(0, 1, 8, 16), T.tq[:, 16:24], x2(1, 1, 8, 16), A.subtract, ["xh0", "xc"], ["xj0"], "xj")
+            tt(x2(0, 1, 16, 24), T.tq[:, 16:24], T.tq[:, 24:32], A.subtract, ["xh0", "xc"], ["xj1"], "xj")
         quant(half(q, 1), half(p, 1), T.vt[:], ["vt%d" % b for b in range(4)], ["q%d1" % k])
         send(k, raw(half(q, 0)), raw(half(q, 1)), "rq%d" % k, ["q%d1" % k])
-        send(k, half(p, 0), half(p, 1), "rp%d" % k, ["q%d1" % k])
+        if k == 3:
+            send(k, half(p, 0), half(p, 1), "rp%d" % k, ["q%d1" % k])
         arrive(k, "ri%d" % k, ["iw%d0" % k])
         arrive(k, "rq%d" % k, ["aq%d" % k])
         arrive(k, "rp%d" % k, ["ap%d" % k])
@@ -377,48 +403,47 @@ def rank_program(g, core, T, topo):
         def relist():
             for h in range(2):
                 for t in range(2):
-                    cp(T.yw[:, 256 * h + 1 + t:256 * h + 256:16], iw[:, 32 * h + 16 * t:32 * h + 16 * t + 16],
+                    ts(T.yw[:, 256 * h + 1 + t:256 * h + 256:16], iw[:, 32 * h + 16 * t:32 * h + 16 * t + 16],
+                       (16.0, 1.0, 0.0625)[k - 1] if t else 1.0, None, A.mult, None,
                        ["iw%d%d" % (k, h), "yw"], ["ya%d%d" % (h, t)], "y%d" % k)
             tr(T.ty[:], T.yw[:], ["ya00", "yw", "yc0"], ["ty"])
 
         if k < 3:
-            cs, cr = T["cs%d" % k], T["cr%d" % k]
+            c0, cr = 64 * k - 64, T["cr%d" % k]
             scores(k, 1, 0, ["q%d1" % k])
+            total(1, half(q, 1), half(p, 1), 128, ["q%d1" % k])
+            act(T.cs[:, c0 + 2:c0 + 64:4], T.rn[:, 0:16], ["sm", "cs"], ["ct%d" % k], scale=0.0, bias=T.sm[:])
+            act(T.hi[:], T.jt[:, 48:64], ["jt3", "sm"], ["hi"], scale=2.0, bias=T.sm[:])
             if k == 1:
-                for t, o in enumerate((A.is_le, A.not_equal)):
-                    ts(half(T.kk, 4 + t), T.rn[:], col(4), FAR, o, A.mult, ["rn", "cg0"], ["kk%d" % (4 + t)], "kk2")
-                ts(T.so[:], T.jr[:, 0:16], 2.0, col(6), A.mult, A.add, ["jr0", "cg2"], ["so"])
-                act(T.jt[:, 32:48], T.jr[:, 16:32], ["jr1", "cg1"], ["jt2"], bias=col(5))
-                act(T.yw[:], T.eb[:, 0:512], ["eb"], ["yw"])
-                act(T.yw[:, 0:512:32], T.jr[:, 0:16], ["jr0", "cg0", "yw"], ["yc0"], bias=col(4), grp="yc")
-                act(T.yw[:, 16:512:32], T.jr[:, 0:16], ["jr0", "cg0", "yw"], ["yc1"], bias=col(4), grp="yc")
+                ts(x2(0, 1, 0, 8), near, turned(3), -2.0, A.is_gt, A.mult, ["tg", "xc"], ["xk"])
+                thresholds(4, col(4), ["cg"])
+                quant(half(T.qx, 1), half(T.px, 1), T.xc[:], ["xc", "xh0", "xj0", "xk"], ["qx1"])
             for b in range(2):
                 unpack(b, 4 + b, half(q, 1), half(p, 1), 128, ["q%d1" % k])
-            flags(k, 0, 0, 4)
-            packed(0)
-            count(0, True, True, None)
+            flags("fl%d" % k, 0, 0, 4)
+            count(1)
             for b in range(2, 4):
                 unpack(b, 4 + b, half(q, 1), half(p, 1), 128, ["q%d1" % k])
             if k == 1:
-                tr(T.tf[:, 64:128], T.ft[:, 64:128], ["ft4"], ["tg"])
+                ts(T.so[:], T.jr[:, 112:128], turned(6), None, A.add, None, ["jr6", "th"], ["so"])
                 quant(T.qv[:], T.pv[:], T.vs[:], ["vs"], ["qv"])
-            cp(cs[:], bank[2][:, 80:128], ["b2"], ["cs%d" % k])
-            send(k, cr[:], cs[:], "rc%d" % k, ["cs%d" % k])
+            cp(T.cs[:, c0 + 1:c0 + 64:2], bank[2][:, 64:96], ["b2", "cs"], ["cs%d" % k])
+            send(k, cr[:], T.cs[:, c0:c0 + 64], "rc%d" % k, ["cs%d" % k, "ct%d" % k])
+            send(k, half(p, 0), half(p, 1), "rp%d" % k, ["q%d1" % k])
             arrive(k, "rc%d" % k, ["cr%d" % k])
             for b in range(4):
                 keep(b, 4 + b, T.fh, 128, 128, ["f%d1"])
-            tt(T.hi[:], bank[2][:, 32:80:3], T.jt[:, 32:48], A.add, ["b2", "jt2"], ["hi"])
-            cp(T.own[:, 2:48:3], bank[2][:, 33:80:3], ["b2"], ["own2"])
+            tt(T.own[:, 0:64:4], bank[2][:, 32:64:2], T.hi[:], A.add, ["b2", "hi"], ["own0"])
+            cp(T.own[:, 2:64:4], bank[2][:, 33:64:2], ["b2"], ["own2"])
             relist()
-            tt(T.own[:, 1:48:3], T.hi[:], T.own[:, 2:48:3], A.subtract, ["hi", "own2"], ["own1"])
             act(T.src[:], T.ty[:].indirect(T.so[:]), ["ty", "so"], ["src"])
             if k == 1:
-                ts(T.fo[:], T.jr[:, 0:16], 0.5, T.tf[:, 64:65], A.mult, A.add, ["jr0", "tg"], ["fo"])
-                ts(T.lo[:], T.jr[:, 32:48], T.tf[:, 96:97], None, A.add, None, ["jr2", "tg"], ["lo"])
+                ts(T.fo[:], T.jr[:, 0:16], 0.5, turned(7), A.mult, A.add, ["jr0", "th"], ["fo"])
+                ts(T.lo[:], T.jr[:, 32:48], turned(8), None, A.add, None, ["jr2", "th"], ["lo"])
             for b in range(4):
                 unpack(b, 4 + b, half(q, 0), half(p, 0), 128, ["aq%d" % k, "ap%d" % k])
                 keep(b, 4 + b, T.fh, 0, 128, ["f%d0"])
-            scan(T.sc[:], T.own[:], cr[:], ["own0", "own1", "own2", "cr%d" % k], ["sc"])
+            scan(T.sc[:], cr[:], T.own[:], ["own0", "own1", "own2", "cr%d" % k], ["sc"])
         else:
             mm(bank[0][:, 0:128], T.qv[:], T.pv[:], half(q, 1), half(p, 1), ["qv", "q31"], ["b0"])
             relist()
@@ -427,18 +452,14 @@ def rank_program(g, core, T, topo):
             dma("y", T.lr[:, 0:256], T.lro[1:128:16, :], ["lro"], ["o0"], "out0")
             dma("y", T.lr[:, 256:512], T.lro[2:128:16, :], ["lro"], ["o1"], "out0")
             mm(bank[1][:, 0:128], T.qv[:], T.pv[:], half(q, 0), half(p, 0), ["qv", "aq3", "ap3"], ["b1"])
-            act(T.pf[:], p[:].indirect(T.fo[:]), ["ap3", "q31", "fo"], ["pf"])
-
-            def codes(h):
-                cp(words(half(T.qf, h)), words(q[:]).indirect(T.fo[:, 8 * h:8 * h + 8]), ["aq3", "q31", "fo"], ["qf%d" % h])
-                dma("y", T.oc[:, 512 * h:512 * h + 512], raw(half(T.qf, h)), ["qf%d" % h], ["o2%d" % h], "out1")
-
-            codes(0)
+            cp(words(T.qf[:]), words(q[:]).indirect(T.fo[:]), ["aq3", "q31", "fo"], ["qf"])
+            dma("y", T.oc[:], raw(T.qf[:]), ["qf"], ["o2"], "out1")
+            act(half(T.pf, 0), p[:].indirect(T.fo[:, 0:8]), ["ap3", "q31", "fo"], ["pf0"])
+            cp(half(T.pf, 1), p[:].indirect(T.fo[:, 8:16]), ["ap3", "q31", "fo"], ["pf1"])
             cp(T.yo[:, 0:256:2], bank[1][:, 0:128], ["b1"], ["yo0"])
             dma("y", T.y[:], T.yo[:], ["yo0", "yo1"], ["o3"], "out1")
-            codes(1)
             for j in range(4):
-                dma("s", T.osc[4 * j:4 * j + 4, :], T.pf[32 * j:32 * j + 4, :], ["pf"], ["o4%d" % j], "out2")
+                dma("s", T.osc[4 * j:4 * j + 4, :], T.pf[32 * j:32 * j + 4, :], ["pf0", "pf1"], ["o4%d" % j], "out2")
     op("y", None, ["o0", "o3", "o40"], [])
     emit(ops, queues, T)
     g.wait_ge(T.sem.sent, sent[0])

@@ -30,6 +30,7 @@ SCRATCH = {
     "src": ("sbuf", [128, 256], BF), "srt": ("sbuf", [128, 288], BF), "tt": ("sbuf", [128, 528], BF),
     "gn": ("sbuf", [128, 16], BF), "lh": ("sbuf", [128, 48], U16),
     "fh": ("sbuf", [128, 1024], BF), "mh": ("sbuf", [128, 1024], BF), "lf": ("sbuf", [128, 512], BF),
+    "mg": ("sbuf", [128, 512], BF),
     "ph": ("sbuf", [128, 512], BF), "p32": ("sbuf", [128, 512], BF), "zt": ("sbuf", [128, 512], BF),
     "qz": ("sbuf", [128, 128], MX), "pz": ("sbuf", [128, 128], U8),
     "v32": ("sbuf", [128, 512], BF), "vt": ("sbuf", [128, 512], BF),
@@ -191,8 +192,8 @@ def rank_program(g, core, T, topo):
     dma("y", T.us[:], T.u[:], [], ["us"])
     dma("y", T.xs[:, 0:512], T.x[:, 0:512], [], ["xs0"])
     dma("y", T.xs[:, 512:1024], T.x[:, 512:1024], [], ["xs1"])
-    dma("y", T.ms[:, 0:512], T.mid[:, 0:512], [], ["ms0"])
-    dma("y", T.ms[:, 512:1024], T.mid[:, 512:1024], [], ["ms1"])
+    dma("y", T.ms[:, 0:512], T.mid[:, 0:512], ["us"], ["ms0"])
+    dma("y", T.ms[:, 512:1024], T.mid[:, 512:1024], ["xs0"], ["ms1"])
 
     x1 = lambda kind, t: T.xc[:, 4 * kind + t:128:8]
     x2 = lambda kind, t, a, b: T.xc[:, 128 + 8 * a + 4 * kind + t:128 + 8 * b:8]
@@ -205,15 +206,16 @@ def rank_program(g, core, T, topo):
     iota(T.jr[:, 96:112], [[1, 16]], 128, 0, ["jr5"])
     dma("y", T.s0[1:128:16, :], T.li[:], ["s0"], ["s0a"], "lists")
     dma("y", T.s0[2:128:16, :], T.ri[:], ["s0"], ["s0b"], "lists")
-    dma("y", T.wp[:], T.ws[:], [], ["wp"], "layer")
+    dma("y", T.wp[:], T.ws[:], ["ms0"], ["wp"], "layer")
     dma("y", raw(T.wq[:]), T.wc[:], [], ["wq"], "layer")
     dma("y", T.vs[:], T.v[:], [], ["vs"])
     for h in range(2):
         iota(T.ft[:, 16 * h:16 + 16 * h], [[0, 2], [32, 4], [128, 2]], 16 * h, 0, ["ft0%d" % h], "ft")
-        iota(T.ft[:, 32 + 16 * h:48 + 16 * h], [[32, 4], [128, 2], [0, 2]], 16 * h, 0, ["ft1%d" % h], "ft")
-        iota(T.ft[:, 64 + 16 * h:72 + 16 * h], [[32, 4], [128, 2]], 16 * h, 0, ["ft2%d" % h], "ft")
-        iota(T.ft[:, 72 + 16 * h:80 + 16 * h], [[2, 4], [8, 2]], 256 + h, 0, ["ft3%d" % h], "ft")
-    iota(T.jr[:, 80:82], [[257, 2]], 1, 0, ["jr4"])
+        iota(T.ft[:, 32 + 16 * h:40 + 16 * h], [[32, 4], [128, 2]], 16 * h, 0, ["ft2%d" % h], "ft")
+        iota(T.ft[:, 40 + 16 * h:48 + 16 * h], [[2, 4], [8, 2]], 256 + h, 0, ["ft3%d" % h], "ft")
+    for h in range(2):
+        iota(T.ft[:, 64 + 16 * h:80 + 16 * h], [[32, 4], [128, 2], [0, 2]], 16 * h, 0, ["ft1%d" % h], "fu0")
+    iota(T.jr[:, 80:82], [[257, 2]], 1, 0, ["jr4"], "fu0")
     for k, pattern in enumerate(([[0, 4], [16, 8]], [[0, 2], [1, 2], [0, 8]], [[0, 2], [1, 16]],
                                  [[16, 2], [32, 8], [8, 2]], [[0, 2], [1, 8], [128, 2]], [[16, 2], [1, 8], [256, 2]])):
         iota(T.ft[:, 96 + 32 * k:128 + 32 * k], pattern, 0, 0, ["fu%d" % k], "fu%d" % (k // 3))
@@ -237,23 +239,22 @@ def rank_program(g, core, T, topo):
     ts(T.eb[:, 3:515:4], T.dg[:], 0.0, None, A.is_equal, None, ["dg", "eb"], ["eb"])
     cp(T.cf[:, 0:4], T.bi[:], ["bi0"], ["cf"])
     cp(T.uo[:], T.jr[:, 0:8], ["jr0"], ["uo"])
-    unit(0)
     ts(x1(1, 1), T.jr[:, 0:16], col(0), 2.0, A.is_gt, A.mult, ["jr0", "cf"], ["xt"], "xd")
     ts(T.tq[:, 0:16], T.jr[:, 0:16], col(0), -512.0, A.is_equal, A.mult, ["jr0", "cf"], ["tq"], "xd")
-    unit(1)
+    unit(0)
     tt(x1(0, 1), T.tq[:, 0:16], x1(1, 1), A.subtract, ["tq", "xt"], ["xv"])
     act(x1(1, 3), x1(1, 1), ["xt"], ["xb0"], grp="xb")
     act(x1(0, 3), x1(0, 1), ["xv"], ["xb1"], grp="xb")
 
-    quant(T.qu[:], T.pu[:], T.us[:], ["us"], ["qu"])
+    unit(1)
     thresholds(0, col(1), ["cf"])
+    quant(T.qu[:], T.pu[:], T.us[:], ["us"], ["qu"])
+    thresholds(2, col(2), ["cf"])
     cp(words(T.qg[:]), words(T.qu[:]).indirect(T.uo[:, 0:8]), ["qu", "uo"], ["qg"])
     act(T.pg[:], T.pu[:].indirect(T.uo[:, 0:8]), ["qu", "uo"], ["pg"])
     act(T.srt[:], T.eb[:, 0:288], ["eb"], ["srt"])
     act(T.jt[:, 0:32:2], T.rn[:, 0:16], ["rn"], ["jt0"], scale=0.0, bias=LOW)
     act(T.jt[:, 32:48], T.jr[:, 96:112], ["jr5", "cf"], ["jt2"], bias=col(0))
-    act(T.yw[:], T.eb[:, 0:512], ["eb"], ["yw"])
-    unit(2)
     quant(half(T.q0, 0), half(T.p0, 0), T.xs[:, 0:512], ["xs0"], ["q00"])
 
     def scores(k, h, bk, r):
@@ -285,41 +286,39 @@ def rank_program(g, core, T, topo):
         keep(b, 4 + b, T.fh, 0, 256, ["f%d0", "f%d1"])
 
     scores(0, 0, 0, ["q00"])
-    unit(3)
-    thresholds(2, col(2), ["cf"])
-    quant(half(T.qx, 0), half(T.px, 0), T.xc[:], ["xc", "xa", "xt", "xv", "xb0"], ["qx0"])
+    unit(2)
     quant(half(T.q0, 1), half(T.p0, 1), T.xs[:, 512:1024], ["xs1"], ["q01"])
     scores(0, 1, 1, ["q01"])
     total(3, T.q0[:], T.p0[:], 256, ["q00", "q01"])
     act(T.jt[:, 1:32:2], T.jt[:, 32:48], ["jt2", "sm"], ["jt1"], scale=2.0, bias=T.sm[:])
+    unit(3)
     flags("fa", 0, 0, 0)
     first(0)
     flags("fa", 2, 1, 2)
+    quant(half(T.qx, 0), half(T.px, 0), T.xc[:], ["xc", "xa", "xt", "xv", "xb0"], ["qx0"])
     count(0)
-    first(1)
-    tr(T.tf[:, 0:96], T.ft[:, 0:96], ["ft00"], ["tf"])
+    first(1), first(2)
     quant(half(T.qm, 0), half(T.pm, 0), T.ms[:, 0:512], ["ms0"], ["qm0"])
-    cp(T.go[:, 0:4:2], T.tf[:, 0:96:64], ["tf"], ["go"])
-    ts(T.go[:, 4:6], T.jr[:, 80:82], turned(1), None, A.add, None, ["tf", "jr4"], ["gp"])
+    tr(T.tf[:, 0:64], T.ft[:, 0:64], ["ft00"], ["tf"])
+    first(3)
     scan(T.sc[:, 0:32], T.jt[:, 0:32], bank[2][:, 0:32], ["b2", "jt0", "jt1"], ["sc"])
+    cp(T.go[:, 0:4:2], T.tf[:, 0:64:32], ["tf"], ["go"])
     fill(T.own[:, 1:64:2], LOW, ["own1"])
-    fill(T.cs[:, 0:128:4], LOW, ["cs"])
     ts(T.po[:], T.sc[:, 1:32:2], 0.5, col(3), A.mult, A.add, ["sc", "cf"], ["po"])
     quant(half(T.qm, 1), half(T.pm, 1), T.ms[:, 512:1024], ["ms1"], ["qm1"])
     iota(T.xc[:, 128:256:4], [[0, 16], [4, 2]], -2, 0, ["xc"], "xg")
     iota(T.xc[:, 256:384:4], [[0, 16], [6, 2]], -4, 0, ["xc"], "xg")
     mbank = (3, 0, 1, 2)
-    first(2), first(3)
     for b in range(4):
         unpack(b, mbank[b], T.qm[:], T.pm[:], 256, ["qm0", "qm1"])
-    for b in range(2):
+    for b in range(3):
         keep(b, mbank[b], T.mh, 0, 256, ["m%d"])
 
     for k in range(1, 4):
         q, p, iw = T["q%d" % k], T["p%d" % k], T["iw%d" % k]
         if k == 1:
             cp(T.srt[:].indirect(T.po[:]), T.s0[:], ["po", "s0a", "s0b"], ["srt"])
-            tr(T.tf[:, 96:192], T.ft[:, 96:192], ["fu0"], ["tg"])
+            tr(T.tf[:, 64:192], T.ft[:, 64:192], ["fu0"], ["tg"])
         else:
             ts(T.po[:], T.sc[:, 3:64:4], 0.5, col(3), A.mult, A.add, ["sc", "cf"], ["po"])
             cp(T.srt[:].indirect(T.po[:]), T.src[:], ["po", "src"], ["srt"])
@@ -330,41 +329,52 @@ def rank_program(g, core, T, topo):
             a = (0, 32, 1, 33)[s]
             tr(half(T.tt, s), T.srt[:, a:a + 255:2], ["srt"], ["tt%d" % s], "tt%d%d" % (k, s // 2))
 
-        turn(0), turn(1), turn(2)
+        turn(0), turn(1), turn(2), turn(3)
         ts(T.lh[:, 0:16], side(0).indirect(T.go[:, 0:1]), 0.0, None, A.add, None, both(0), ["lh0"])
-        turn(3)
         if k == 1:
             ts(T.gn[:], T.tt[:, 2:256:16], 16.0, None, A.mult, None, both(0), ["gn"])
-            ts(T.lh[:, 16:32], side(1).indirect(T.go[:, 0:1]), 0.0, None, A.add, None, both(1), ["lh1"])
+        ts(T.lh[:, 16:32], side(1).indirect(T.go[:, 0:1]), 0.0, None, A.add, None, both(1), ["lh1"])
+        if k == 1:
+            ts(T.go[:, 4:6], T.jr[:, 80:82], turned(2), None, A.add, None, ["tg"], ["gp"])
             tt(T.tt[:, 512:528], T.gn[:], T.tt[:, 257:512:16], A.add, both(1) + ["gn"], ["tt4"])
         else:
             tt(T.tt[:, 512:528], T.tt[:, 2:256:16], T.tt[:, 257:512:16], A.add, both(0) + both(1), ["tt4"])
-            ts(T.lh[:, 16:32], side(1).indirect(T.go[:, 0:1]), 0.0, None, A.add, None, both(1), ["lh1"])
+        cp(half(T.lf, 1), T.fh[:, 256:512].indirect(T.lh[:, 0:8]), ["lh0", "f10", "f11"], ["lf1"])
         ts(T.lh[:, 32:48], T.tt[:, 256:528].indirect(T.go[:, 2:3]), 0.0, None, A.add, None, both(1) + ["tt4"], ["no"])
-        for b in range(4):
-            act(half(T.lf, b), T.fh[:, 256 * b:256 * b + 256].indirect(T.lh[:, 0:8]),
-                ["lh0", "f%d0" % b, "f%d1" % b], ["lf%d" % b])
-            if b == 1:
+        plan = "l0 l2 i0 l3 m3 g2 g3" if k == 1 else "l0 l2 l3 g1 g2 g3 i0"
+        aside = [int(x[1]) for x in plan.split() if x[0] == "g"]
+        for x in plan.split():
+            b = int(x[1])
+            if x[0] == "l":
+                act(half(T.lf, b), T.fh[:, 256 * b:256 * b + 256].indirect(T.lh[:, 0:8]),
+                    ["lh0", "f%d0" % b, "f%d1" % b], ["lf%d" % b])
+            elif x[0] == "g":
+                act(half(T.mg, b), T.mh[:, 256 * b:256 * b + 256].indirect(T.lh[:, 40:48]), ["no", "m%d" % b], ["mg%d" % b])
+            elif x[0] == "m":
+                keep(b, mbank[b], T.mh, 0, 256, ["m%d"])
+            else:
                 act(iw[:, 32:64], T.tt[:, 0:512].indirect(T.go[:, 4:6]), both(0) + both(1) + ["gp"], ["iw%d1" % k])
                 send(k, iw[:, 0:32], iw[:, 32:64], "ri%d" % k, ["iw%d1" % k])
-        if k == 1:
-            for b in range(2, 4):
-                keep(b, mbank[b], T.mh, 0, 256, ["m%d"])
 
         def larger(b):
             tt(half(T.ph, b), T.fh[:, 256 * b:256 * b + 256].indirect(T.lh[:, 16:24]), half(T.lf, b), A.max,
                ["lh1", "lf%d" % b, "f%d0" % b, "f%d1" % b], ["ph%d" % b])
-            if b % 2:
+            if b % 2 and k == 1:
                 act(T.p32[:, 128 * b - 128:128 * b + 128], T.ph[:, 128 * b - 128:128 * b + 128], ["ph%d" % (b - 1), "ph%d" % b],
                     ["p32%d" % (b - 1), "p32%d" % b], scale=64.0)
 
         def middle(b):
+            if b in aside:
+                tt(T.zt[:, b:512:4], half(T.mg, b), half(T.ph, b), A.add, ["mg%d" % b, "ph%d" % b], ["zt%d" % b], "zt%d" % k)
+                return
             tt(T.zt[:, b:512:4], T.mh[:, 256 * b:256 * b + 256].indirect(T.lh[:, 40:48]), half(T.ph, b), A.add,
                ["no", "m%d" % b, "ph%d" % b], ["zt%d" % b], "zt%d" % k)
 
-        larger(0), larger(1), middle(0), larger(2), middle(1), larger(3), middle(2), middle(3)
+        larger(0), larger(1), middle(0), larger(2), larger(3), middle(1), middle(2), middle(3)
         if k == 1:
+            fill(T.cs[:, 0:128:4], LOW, ["cs"])
             tr(T.tf[:, 192:288], T.ft[:, 192:288], ["fu3"], ["th"])
+            act(T.yw[:], T.eb[:, 0:512], ["eb"], ["yw"])
             act(T.jt[:, 48:64], T.jr[:, 16:32], ["jr1", "cf"], ["jt3"], bias=col(0))
         quant(T.qz[:], T.pz[:], T.zt[:], ["zt%d" % b for b in range(4)], ["qz"])
         for b in range(4):
@@ -377,6 +387,10 @@ def rank_program(g, core, T, topo):
             ts(T.tq[:, 24:32], near, turned(3), 4.0, A.is_gt, A.mult, ["tg"], ["xh2"], "xh")
             ts(x2(1, 1, 24, 32), near, turned(3), 2.0, A.is_ge, A.mult, ["tg", "xc"], ["xh3"], "xh")
             ts(x2(0, 1, 24, 32), near, turned(3), -4.0, A.is_ge, A.mult, ["tg", "xc"], ["xh4"], "xh")
+        else:
+            for h in range(2):
+                ts(T.p32[:, 256 * h:256 * h + 256], T.ph[:, 256 * h:256 * h + 256], 64.0, None, A.mult, None,
+                   ["ph%d" % (2 * h), "ph%d" % (2 * h + 1)], ["p32%d" % (2 * h), "p32%d" % (2 * h + 1)])
 
         def add(b):
             tt(half(T.v32, b), bank[4 + b][:, 0:128], half(T.p32, b), A.add, ["b%d" % (4 + b), "p32%d" % b], ["v32%d" % b])
@@ -452,14 +466,14 @@ def rank_program(g, core, T, topo):
             dma("y", T.lr[:, 0:256], T.lro[1:128:16, :], ["lro"], ["o0"], "out0")
             dma("y", T.lr[:, 256:512], T.lro[2:128:16, :], ["lro"], ["o1"], "out0")
             mm(bank[1][:, 0:128], T.qv[:], T.pv[:], half(q, 0), half(p, 0), ["qv", "aq3", "ap3"], ["b1"])
-            cp(words(T.qf[:]), words(q[:]).indirect(T.fo[:]), ["aq3", "q31", "fo"], ["qf"])
-            dma("y", T.oc[:], raw(T.qf[:]), ["qf"], ["o2"], "out1")
-            act(half(T.pf, 0), p[:].indirect(T.fo[:, 0:8]), ["ap3", "q31", "fo"], ["pf0"])
-            cp(half(T.pf, 1), p[:].indirect(T.fo[:, 8:16]), ["ap3", "q31", "fo"], ["pf1"])
+            for h in range(2):
+                cp(words(half(T.qf, h)), words(q[:]).indirect(T.fo[:, 8 * h:8 * h + 8]), ["aq3", "q31", "fo"], ["qf%d" % h])
+                dma("y", T.oc[:, 512 * h:512 * h + 512], raw(half(T.qf, h)), ["qf%d" % h], ["o2%d" % h], "out1")
+            act(T.pf[:], p[:].indirect(T.fo[:]), ["ap3", "q31", "fo"], ["pf"])
             cp(T.yo[:, 0:256:2], bank[1][:, 0:128], ["b1"], ["yo0"])
             dma("y", T.y[:], T.yo[:], ["yo0", "yo1"], ["o3"], "out1")
             for j in range(4):
-                dma("s", T.osc[4 * j:4 * j + 4, :], T.pf[32 * j:32 * j + 4, :], ["pf0", "pf1"], ["o4%d" % j], "out2")
+                dma("sssy"[j], T.osc[4 * j:4 * j + 4, :], T.pf[32 * j:32 * j + 4, :], ["pf"], ["o4%d" % j], "out2")
     op("y", None, ["o0", "o3", "o40"], [])
     emit(ops, queues, T)
     g.wait_ge(T.sem.sent, sent[0])

from concourse.mybir import dt, AluOpType, ActivationFunctionType

BF, F32, I32, U16, U8, MX = "bfloat16", "float32", "int32", "uint16", "uint8", "float8_e4m3fn_x4"
DIST = [1, 2, 4]
FAR = float(2 ** 80)
TINY = float(2.0 ** -110)
LOW = -4096.0

SCRATCH = {
    "xs": ("sbuf", [128, 1024], BF), "us": ("sbuf", [128, 512], BF), "ms": ("sbuf", [128, 1024], BF),
    "vs": ("sbuf", [128, 512], BF), "s0": ("sbuf", [128, 256], I32),
    "wq": ("sbuf", [128, 512], MX), "wp": ("sbuf", [128, 512], U8),
    "qu": ("sbuf", [128, 128], MX), "pu": ("sbuf", [128, 128], U8),
    "qg": ("sbuf", [128, 128], MX), "pg": ("sbuf", [128, 128], U8),
    "qv": ("sbuf", [128, 128], MX), "pv": ("sbuf", [128, 128], U8),
    "qm": ("sbuf", [128, 256], MX), "pm": ("sbuf", [128, 256], U8),
    "ip": ("sbuf", [128, 2], I32), "bi": ("sbuf", [128, 4], I32), "cf": ("sbuf", [128, 8], F32),
    "rn": ("sbuf", [128, 128], BF), "dg": ("sbuf", [128, 128], BF), "jr": ("sbuf", [128, 128], F32),
    "tq": ("sbuf", [128, 32], BF),
    "eb": ("sbuf", [128, 516], BF), "qe": ("sbuf", [128, 512], MX), "pe": ("sbuf", [128, 512], U8),
    "kk": ("sbuf", [128, 768], BF),
    "xc": ("sbuf", [128, 512], BF), "qx": ("sbuf", [128, 256], MX), "px": ("sbuf", [128, 256], U8),
    "jt": ("sbuf", [128, 64], F32), "ft": ("sbuf", [128, 288], F32), "tf": ("sbuf", [128, 288], F32),
    "uo": ("sbuf", [128, 8], U16), "so": ("sbuf", [128, 16], U16), "go": ("sbuf", [128, 8], U16),
    "fo": ("sbuf", [128, 16], U16), "lo": ("sbuf", [128, 16], U16),
    "wf": ("sbuf", [128, 512], BF), "qw": ("sbuf", [128, 128], MX), "pw": ("sbuf", [128, 128], U8),
    "sg": ("sbuf", [128, 256], BF), "sm": ("sbuf", [128, 1], F32), "cs": ("sbuf", [128, 128], BF),
    "hi": ("sbuf", [128, 16], F32), "own": ("sbuf", [128, 64], F32), "sc": ("sbuf", [128, 64], F32),
    "po": ("sbuf", [128, 16], U16), "yw": ("sbuf", [128, 512], BF), "ty": ("sbuf", [128, 512], BF),
    "src": ("sbuf", [128, 256], BF), "srt": ("sbuf", [128, 288], BF), "tt": ("sbuf", [128, 528], BF),
    "gn": ("sbuf", [128, 16], BF), "lh": ("sbuf", [128, 48], U16),
    "fh": ("sbuf", [128, 1024], BF), "mh": ("sbuf", [128, 1024], BF), "lf": ("sbuf", [128, 512], BF),
    "mg": ("sbuf", [128, 512], BF),
    "ph": ("sbuf", [128, 512], BF), "p32": ("sbuf", [128, 512], BF), "zt": ("sbuf", [128, 512], BF),
    "qz": ("sbuf", [128, 128], MX), "pz": ("sbuf", [128, 128], U8),
    "v32": ("sbuf", [128, 512], BF), "vt": ("sbuf", [128, 512], BF),
    "qf": ("sbuf", [128, 256], MX), "pf": ("sbuf", [128, 256], U8),
    "yo": ("sbuf", [128, 256], F32), "lro": ("sbuf", [128, 256], F32),
}
for _k in range(4):
    SCRATCH["q%d" % _k] = ("sbuf", [128, 256], MX)
    SCRATCH["p%d" % _k] = ("sbuf", [128, 256], U8)
for _k in range(1, 4):
    SCRATCH["iw%d" % _k] = ("sbuf", [128, 64], BF)
for _k in range(1, 3):
    SCRATCH["cr%d" % _k] = ("sbuf", [128, 64], BF)
for _k in range(8):
    SCRATCH["b%d" % _k] = ("psum", [128, 512], F32)

POOL = {"v": 56, "s": 30, "t": 20, "g": 14, "d": 14}
ARRIVE = ["ri1", "ri2", "ri3", "rq1", "rq2", "rq3", "rp1", "rp2", "rp3", "rc1", "rc2"]
SEMAPHORES = ["%s%d" % (q, i) for q in POOL for i in range(POOL[q])] + ARRIVE + ["sent"]


def emit(ops, queues, T):
    size, last = {}, {}
    for i, o in enumerate(ops):
        size[o["grp"]] = size.get(o["grp"], 0) + o["inc"]
        last[o["grp"]] = i
    writer, readers, known, seen, waits, wanted, before = {}, {}, {}, {}, [], set(), []
    for i, o in enumerate(ops):
        need = []
        for t in o["r"] + o["w"]:
            if t in writer:
                need.append(writer[t])
        for t in o["w"]:
            need += readers.get(t, [])
        kn = known.setdefault(o["q"], set())
        mine = []
        for x in sorted(set(need), key=lambda x: -last[x]):
            if x != o["grp"] and x not in kn:
                assert last[x] < i, (x, o["grp"])
                mine.append(x)
                kn.add(x)
                kn.update(seen[x])
        waits.append(mine)
        wanted.update(mine)
        before.append(set(kn))
        seen.setdefault(o["grp"], set()).update(kn)
        for t in o["r"]:
            if o["hold"]:
                readers.setdefault(t, []).append(o["grp"])
        for t in o["w"]:
            writer[t] = o["grp"]
            readers[t] = []
    turn, count, user, place = {}, {}, {}, {}
    for i, o in enumerate(ops):
        x = o["grp"]
        if o["sem"] is not None:
            place[x] = (o["sem"], size[x])
            continue
        e = queues[o["q"]]
        for y in waits[i]:
            e.wait_ge(T.sem[place[y][0]], place[y][1])
        if o["fn"] is None:
            continue
        if x in wanted and x not in place:
            pool = o["pool"]
            n = turn.get(pool, 0)
            turn[pool] = n + 1
            name = "%s%d" % (pool, n % POOL[pool])
            if name in user and user[name] not in before[i]:
                e.wait_ge(T.sem[name], count[name])
            user[name] = x
            count[name] = count.get(name, 0) + size[x]
            place[x] = (name, count[name])
        ins = o["fn"]()
        if x in wanted:
            ins.then_inc(T.sem[place[x][0]], o["inc"])


def rank_program(g, core, T, topo):
    rank = T.rank_of(core)
    if rank is None:
        return
    n_ranks = len(T.cores)
    A, ACT = AluOpType, ActivationFunctionType
    vec, sca, ten = g.vector, g.scalar, g.tensor
    queues = {"v": vec, "s": sca, "t": ten, "g": g, "y": g.sync}
    ops = []

    def op(q, fn, r, w, grp=None, pool=None, inc=1, hold=True, sem=None):
        ops.append({"q": q, "fn": fn, "r": list(r), "w": list(w), "grp": grp or "op%d" % len(ops),
                    "pool": pool or q, "inc": inc, "hold": hold, "sem": sem})

    def dma(q, out, in_, r, w, grp=None):
        op(q, lambda: queues[q].dma_start(out, in_), r, w, grp, pool="d", inc=16)

    def ts(out, in0, s1, s2, o0, o1, r, w, grp=None):
        if s2 is None:
            op("v", lambda: vec.tensor_scalar(out, in0, s1, None, o0), r, w, grp)
        else:
            op("v", lambda: vec.tensor_scalar(out, in0, s1, s2, o0, o1), r, w, grp)

    def tt(out, in0, in1, o, r, w, grp=None):
        op("v", lambda: vec.tensor_tensor(out, in0, in1, o), r, w, grp)

    def cp(out, in_, r, w, grp=None):
        op("v", lambda: vec.tensor_copy(out, in_), r, w, grp)

    def tr(out, in_, r, w, grp=None):
        op("v", lambda: vec.transpose(out, in_), r, w, grp)

    def scan(out, d0, d1, r, w):
        op("v", lambda: vec.tensor_tensor_scan(out, d0, d1, 0.0, A.add, A.max), r, w)

    def fill(out, c, w, grp=None):
        op("v", lambda: vec.memset(out, c), [], w, grp)

    def quant(q, p, in_, r, w, grp=None):
        op("v", lambda: vec.quantize_mx(q, p, in_), r, w, grp)

    def act(out, in_, r, w, scale=None, bias=None, grp=None):
        if bias is not None:
            op("s", lambda: sca.activation(out, in_, ACT.Identity, bias=bias, scale=1.0 if scale is None else scale), r, w, grp)
        elif scale is not None:
            op("s", lambda: sca.activation(out, in_, ACT.Copy, scale=scale), r, w, grp)
        else:
            op("s", lambda: sca.activation(out, in_, ACT.Copy), r, w, grp)

    def mm(out, lq, lp, rq, rp, r, w):
        op("t", lambda: ten.matmul_mx(out, lq, lp, rq, rp, True, True), r, w)

    def iota(out, pattern, base, cm, w, grp=None, whole=False):
        if whole:
            op("g", lambda: g.iota(out, pattern, base, cm), [], w, grp)
        else:
            op("g", lambda: g.iota(out, pattern, base, cm, allow_small_or_imprecise_dtypes=True), [], w, grp)

    sent = [0]

    def send(k, out, in_, sem, r):
        dst = T.cores[(rank + DIST[k - 1]) % n_ranks]
        rid, pid, _ = topo.addr(dst)
        mask = topo.mask(core, dst)
        sent[0] += len(topo.engines(core, dst))
        op("g", lambda: g.remote_dma(out, in_, T.sem[sem], T.sem.sent, pid, rid, mask), r, [], hold=False)

    def arrive(k, sem, w):
        src = T.cores[(rank - DIST[k - 1]) % n_ranks]
        op("x", None, [], w, inc=len(topo.engines(src, core)), sem=sem)

    bank = [T["b%d" % k] for k in range(8)]
    col = lambda c: T.cf[:, c:c + 1]
    turned = lambda k: T.tf[:, 32 * k:32 * k + 1]
    words = lambda v: v.bitcast(dt.uint32)
    raw = lambda v: v.bitcast(dt.uint8)

    def half(t, h):
        return t[:, 128 * h:128 * h + 128]

    dma("y", T.us[:], T.u[:], [], ["us"])
    dma("y", T.xs[:, 0:512], T.x[:, 0:512], [], ["xs0"])
    dma("y", T.xs[:, 512:1024], T.x[:, 512:1024], [], ["xs1"])
    dma("y", T.ms[:, 0:512], T.mid[:, 0:512], ["us"], ["ms0"])
    dma("y", T.ms[:, 512:1024], T.mid[:, 512:1024], ["xs0"], ["ms1"])

    x1 = lambda kind, t: T.xc[:, 4 * kind + t:128:8]
    x2 = lambda kind, t, a, b: T.xc[:, 128 + 8 * a + 4 * kind + t:128 + 8 * b:8]
    iota(T.ip[:], [[2048, 2]], 0, 16, ["ip"], whole=True)
    iota(T.dg[:], [[1, 128]], 0, -1, ["dg"])
    iota(T.jr[:, 0:16], [[16, 16]], 0, 0, ["jr0"])
    iota(T.rn[:], [[0, 8], [1, 16]], 0, 0, ["rn"])
    iota(T.xc[:, 0:128:2], [[0, 16], [4, 2], [0, 2]], -2, 0, ["xa"])
    iota(T.s0[:], [[1, 16], [16, 16]], 0, 0, ["s0"], whole=True)
    iota(T.jr[:, 96:112], [[1, 16]], 128, 0, ["jr5"])
    dma("y", T.s0[1:128:16, :], T.li[:], ["s0"], ["s0a"], "lists")
    dma("y", T.s0[2:128:16, :], T.ri[:], ["s0"], ["s0b"], "lists")
    dma("y", T.wp[:], T.ws[:], ["ms0"], ["wp"], "layer")
    dma("y", raw(T.wq[:]), T.wc[:], [], ["wq"], "layer")
    dma("y", T.vs[:], T.v[:], [], ["vs"])
    for h in range(2):
        iota(T.ft[:, 16 * h:16 + 16 * h], [[0, 2], [32, 4], [128, 2]], 16 * h, 0, ["ft0%d" % h], "ft")
        iota(T.ft[:, 32 + 16 * h:40 + 16 * h], [[32, 4], [128, 2]], 16 * h, 0, ["ft2%d" % h], "ft")
        iota(T.ft[:, 40 + 16 * h:48 + 16 * h], [[2, 4], [8, 2]], 256 + h, 0, ["ft3%d" % h], "ft")
    for h in range(2):
        iota(T.ft[:, 64 + 16 * h:80 + 16 * h], [[32, 4], [128, 2], [0, 2]], 16 * h, 0, ["ft1%d" % h], "fu0")
    iota(T.jr[:, 80:82], [[257, 2]], 1, 0, ["jr4"], "fu0")
    for k, pattern in enumerate(([[0, 4], [16, 8]], [[0, 2], [1, 2], [0, 8]], [[0, 2], [1, 16]],
                                 [[16, 2], [32, 8], [8, 2]], [[0, 2], [1, 8], [128, 2]], [[16, 2], [1, 8], [256, 2]])):
        iota(T.ft[:, 96 + 32 * k:128 + 32 * k], pattern, 0, 0, ["fu%d" % k], "fu%d" % (k // 3))
    iota(T.jr[:, 48:72], [[0, 3], [16, 8]], 0, 0, ["jr3"], "fv")
    iota(T.jr[:, 16:32], [[1, 2], [2, 8]], 128, 0, ["jr1"], "fv")
    iota(T.jr[:, 32:48], [[32, 8], [8, 2]], 0, 0, ["jr2"], "fv")
    iota(T.jr[:, 112:128], [[256, 2], [1, 8]], 0, 0, ["jr6"], "fv")

    def unit(b):
        quant(half(T.qe, b), half(T.pe, b), T.eb[:, 3 - b:515 - b], ["eb"], ["qe%d" % b])

    def thresholds(c, block, r):
        for t, o in enumerate((A.is_le, A.not_equal)):
            ts(half(T.kk, c + t), T.rn[:], block, FAR, o, A.mult, ["rn"] + r, ["kk%d" % (c + t)], "kk%d" % c)

    fill(T.eb[:], 0.0, ["eb"])
    fill(T.xc[:, 128:512], 0.0, ["xc"])
    ts(T.bi[:, 0:1], T.ip[:, 0:1], 255, None, A.bitwise_and, None, ["ip"], ["bi0"], "bi")
    ts(T.bi[:, 1:3], T.ip[:], 8, None, A.arith_shift_right, None, ["ip"], ["bi1"], "bi")
    ts(T.bi[:, 3:4], T.ip[:, 0:1], 3, 32, A.arith_shift_right, A.bitwise_and, ["ip"], ["bi2"], "bi")
    ts(T.eb[:, 3:515:4], T.dg[:], 0.0, None, A.is_equal, None, ["dg", "eb"], ["eb"])
    cp(T.cf[:, 0:4], T.bi[:], ["bi0"], ["cf"])
    cp(T.uo[:], T.jr[:, 0:8], ["jr0"], ["uo"])
    ts(x1(1, 1), T.jr[:, 0:16], col(0), 2.0, A.is_gt, A.mult, ["jr0", "cf"], ["xt"], "xd")
    ts(T.tq[:, 0:16], T.jr[:, 0:16], col(0), -512.0, A.is_equal, A.mult, ["jr0", "cf"], ["tq"], "xd")
    unit(0)
    tt(x1(0, 1), T.tq[:, 0:16], x1(1, 1), A.subtract, ["tq", "xt"], ["xv"])
    act(x1(1, 3), x1(1, 1), ["xt"], ["xb0"], grp="xb")
    act(x1(0, 3), x1(0, 1), ["xv"], ["xb1"], grp="xb")

    unit(1)
    thresholds(0, col(1), ["cf"])
    quant(T.qu[:], T.pu[:], T.us[:], ["us"], ["qu"])
    thresholds(2, col(2), ["cf"])
    cp(words(T.qg[:]), words(T.qu[:]).indirect(T.uo[:, 0:8]), ["qu", "uo"], ["qg"])
    act(T.pg[:], T.pu[:].indirect(T.uo[:, 0:8]), ["qu", "uo"], ["pg"])
    act(T.srt[:], T.eb[:, 0:288], ["eb"], ["srt"])
    act(T.jt[:, 0:32:2], T.rn[:, 0:16], ["rn"], ["jt0"], scale=0.0, bias=LOW)
    act(T.jt[:, 32:48], T.jr[:, 96:112], ["jr5", "cf"], ["jt2"], bias=col(0))
    quant(half(T.q0, 0), half(T.p0, 0), T.xs[:, 0:512], ["xs0"], ["q00"])

    def scores(k, h, bk, r):
        mm(bank[bk][:, 0:128], half(T["q%d" % k], h), half(T["p%d" % k], h), T.qg[:], T.pg[:],
           r + ["qg", "pg"], ["b%d" % bk])

    def total(bk, q, p, n, r):
        mm(bank[bk][:, 0:n], T.qg[:], T.pg[:], q, p, r + ["qg", "pg"], ["b%d" % bk])
        op("s", lambda: sca.activation(T.sg[:, 0:n], bank[bk][:, 0:n], ACT.Sign, bias=-TINY, accum_out=T.sm[:]),
           ["b%d" % bk], ["sm"])

    def flags(grp, slot, bk, kk):
        for t in range(2):
            tt(T.wf[:, slot + t:512:4], bank[bk][:, 0:128], half(T.kk, kk + t), A.is_gt,
               ["b%d" % bk, "kk%d" % (kk + t)], ["w%d" % (slot + t)], grp)

    def count(x):
        quant(T.qw[:], T.pw[:], T.wf[:], ["w%d" % t for t in range(4)], ["qw"])
        mm(bank[2][:, 0:128], T.qw[:], T.pw[:], half(T.qx, x), half(T.px, x), ["qw", "qx%d" % x], ["b2"])

    def unpack(b, bk, q, p, n, r):
        mm(bank[bk][:, 0:n], half(T.qe, b), half(T.pe, b), q, p, r + ["qe%d" % b], ["b%d" % bk])

    def keep(b, bk, dst, c, n, w):
        act(dst[:, 256 * b + c:256 * b + c + n], bank[bk][:, 0:n], ["b%d" % bk], [x % b for x in w], scale=0.5)

    def first(b):
        unpack(b, 4 + b, T.q0[:], T.p0[:], 256, ["q00", "q01"])
        keep(b, 4 + b, T.fh, 0, 256, ["f%d0", "f%d1"])

    scores(0, 0, 0, ["q00"])
    unit(2)
    quant(half(T.q0, 1), half(T.p0, 1), T.xs[:, 512:1024], ["xs1"], ["q01"])
    scores(0, 1, 1, ["q01"])
    total(3, T.q0[:], T.p0[:], 256, ["q00", "q01"])
    act(T.jt[:, 1:32:2], T.jt[:, 32:48], ["jt2", "sm"], ["jt1"], scale=2.0, bias=T.sm[:])
    unit(3)
    flags("fa", 0, 0, 0)
    first(0)
    flags("fa", 2, 1, 2)
    quant(half(T.qx, 0), half(T.px, 0), T.xc[:], ["xc", "xa", "xt", "xv", "xb0"], ["qx0"])
    count(0)
    first(1), first(2)
    quant(half(T.qm, 0), half(T.pm, 0), T.ms[:, 0:512], ["ms0"], ["qm0"])
    tr(T.tf[:, 0:64], T.ft[:, 0:64], ["ft00"], ["tf"])
    first(3)
    scan(T.sc[:, 0:32], T.jt[:, 0:32], bank[2][:, 0:32], ["b2", "jt0", "jt1"], ["sc"])
    cp(T.go[:, 0:4:2], T.tf[:, 0:64:32], ["tf"], ["go"])
    fill(T.own[:, 1:64:2], LOW, ["own1"])
    ts(T.po[:], T.sc[:, 1:32:2], 0.5, col(3), A.mult, A.add, ["sc", "cf"], ["po"])
    quant(half(T.qm, 1), half(T.pm, 1), T.ms[:, 512:1024], ["ms1"], ["qm1"])
    iota(T.xc[:, 128:256:4], [[0, 16], [4, 2]], -2, 0, ["xc"], "xg")
    iota(T.xc[:, 256:384:4], [[0, 16], [6, 2]], -4, 0, ["xc"], "xg")
    mbank = (3, 0, 1, 2)
    for b in range(4):
        unpack(b, mbank[b], T.qm[:], T.pm[:], 256, ["qm0", "qm1"])
    for b in range(3):
        keep(b, mbank[b], T.mh, 0, 256, ["m%d"])

    for k in range(1, 4):
        q, p, iw = T["q%d" % k], T["p%d" % k], T["iw%d" % k]
        if k == 1:
            cp(T.srt[:].indirect(T.po[:]), T.s0[:], ["po", "s0a", "s0b"], ["srt"])
            tr(T.tf[:, 64:192], T.ft[:, 64:192], ["fu0"], ["tg"])
        else:
            ts(T.po[:], T.sc[:, 3:64:4], 0.5, col(3), A.mult, A.add, ["sc", "cf"], ["po"])
            cp(T.srt[:].indirect(T.po[:]), T.src[:], ["po", "src"], ["srt"])
        side = lambda j: T.tt[:, 256 * j:256 * j + 256]
        both = lambda j: ["tt%d" % (2 * j), "tt%d" % (2 * j + 1), "go"]

        def turn(s):
            a = (0, 32, 1, 33)[s]
            tr(half(T.tt, s), T.srt[:, a:a + 255:2], ["srt"], ["tt%d" % s], "tt%d%d" % (k, s // 2))

        turn(0), turn(1), turn(2), turn(3)
        ts(T.lh[:, 0:16], side(0).indirect(T.go[:, 0:1]), 0.0, None, A.add, None, both(0), ["lh0"])
        if k == 1:
            ts(T.gn[:], T.tt[:, 2:256:16], 16.0, None, A.mult, None, both(0), ["gn"])
        ts(T.lh[:, 16:32], side(1).indirect(T.go[:, 0:1]), 0.0, None, A.add, None, both(1), ["lh1"])
        if k == 1:
            ts(T.go[:, 4:6], T.jr[:, 80:82], turned(2), None, A.add, None, ["tg"], ["gp"])
            tt(T.tt[:, 512:528], T.gn[:], T.tt[:, 257:512:16], A.add, both(1) + ["gn"], ["tt4"])
        else:
            tt(T.tt[:, 512:528], T.tt[:, 2:256:16], T.tt[:, 257:512:16], A.add, both(0) + both(1), ["tt4"])
        cp(half(T.lf, 1), T.fh[:, 256:512].indirect(T.lh[:, 0:8]), ["lh0", "f10", "f11"], ["lf1"])
        ts(T.lh[:, 32:48], T.tt[:, 256:528].indirect(T.go[:, 2:3]), 0.0, None, A.add, None, both(1) + ["tt4"], ["no"])
        plan = "l0 l2 i0 l3 m3 g2 g3" if k == 1 else "l0 l2 l3 g1 g2 g3 i0"
        aside = [int(x[1]) for x in plan.split() if x[0] == "g"]
        for x in plan.split():
            b = int(x[1])
            if x[0] == "l":
                act(half(T.lf, b), T.fh[:, 256 * b:256 * b + 256].indirect(T.lh[:, 0:8]),
                    ["lh0", "f%d0" % b, "f%d1" % b], ["lf%d" % b])
            elif x[0] == "g":
                act(half(T.mg, b), T.mh[:, 256 * b:256 * b + 256].indirect(T.lh[:, 40:48]), ["no", "m%d" % b], ["mg%d" % b])
            elif x[0] == "m":
                keep(b, mbank[b], T.mh, 0, 256, ["m%d"])
            else:
                act(iw[:, 32:64], T.tt[:, 0:512].indirect(T.go[:, 4:6]), both(0) + both(1) + ["gp"], ["iw%d1" % k])
                send(k, iw[:, 0:32], iw[:, 32:64], "ri%d" % k, ["iw%d1" % k])

        def larger(b):
            tt(half(T.ph, b), T.fh[:, 256 * b:256 * b + 256].indirect(T.lh[:, 16:24]), half(T.lf, b), A.max,
               ["lh1", "lf%d" % b, "f%d0" % b, "f%d1" % b], ["ph%d" % b])
            if b % 2 and k == 1:
                act(T.p32[:, 128 * b - 128:128 * b + 128], T.ph[:, 128 * b - 128:128 * b + 128], ["ph%d" % (b - 1), "ph%d" % b],
                    ["p32%d" % (b - 1), "p32%d" % b], scale=64.0)

        def middle(b):
            if b in aside:
                tt(T.zt[:, b:512:4], half(T.mg, b), half(T.ph, b), A.add, ["mg%d" % b, "ph%d" % b], ["zt%d" % b], "zt%d" % k)
                return
            tt(T.zt[:, b:512:4], T.mh[:, 256 * b:256 * b + 256].indirect(T.lh[:, 40:48]), half(T.ph, b), A.add,
               ["no", "m%d" % b, "ph%d" % b], ["zt%d" % b], "zt%d" % k)

        larger(0), larger(1), middle(0), larger(2), larger(3), middle(1), middle(2), middle(3)
        if k == 1:
            fill(T.cs[:, 0:128:4], LOW, ["cs"])
            tr(T.tf[:, 192:288], T.ft[:, 192:288], ["fu3"], ["th"])
            act(T.yw[:], T.eb[:, 0:512], ["eb"], ["yw"])
            act(T.jt[:, 48:64], T.jr[:, 16:32], ["jr1", "cf"], ["jt3"], bias=col(0))
        quant(T.qz[:], T.pz[:], T.zt[:], ["zt%d" % b for b in range(4)], ["qz"])
        for b in range(4):
            mm(bank[4 + b][:, 0:128], half(T.wq, b), half(T.wp, b), T.qz[:], T.pz[:], ["wq", "wp", "qz"], ["b%d" % (4 + b)])
        if k == 1:
            near = T.jr[:, 48:56]
            ts(col(4), col(1), 2.0, turned(4), A.mult, A.add, ["cf", "tg"], ["cg"])
            ts(x2(1, 1, 0, 24), T.jr[:, 48:72], turned(3), 2.0, A.is_gt, A.mult, ["tg", "jr3", "xc"], ["xh0"], "xh")
            ts(T.tq[:, 16:24], near, turned(3), -512.0, A.is_equal, A.mult, ["tg"], ["xh1"], "xh")
            ts(T.tq[:, 24:32], near, turned(3), 4.0, A.is_gt, A.mult, ["tg"], ["xh2"], "xh")
            ts(x2(1, 1, 24, 32), near, turned(3), 2.0, A.is_ge, A.mult, ["tg", "xc"], ["xh3"], "xh")
            ts(x2(0, 1, 24, 32), near, turned(3), -4.0, A.is_ge, A.mult, ["tg", "xc"], ["xh4"], "xh")
        else:
            for h in range(2):
                ts(T.p32[:, 256 * h:256 * h + 256], T.ph[:, 256 * h:256 * h + 256], 64.0, None, A.mult, None,
                   ["ph%d" % (2 * h), "ph%d" % (2 * h + 1)], ["p32%d" % (2 * h), "p32%d" % (2 * h + 1)])

        def add(b):
            tt(half(T.v32, b), bank[4 + b][:, 0:128], half(T.p32, b), A.add, ["b%d" % (4 + b), "p32%d" % b], ["v32%d" % b])

        def small(b):
            ts(T.vt[:, b:512:4], half(T.v32, b), 0.03125, None, A.mult, None, ["v32%d" % b], ["vt%d" % b])

        add(0)
        act(T.vt[:, 0:512:4], half(T.v32, 0), ["v320"], ["vt0"], scale=0.03125)
        add(1), add(2), add(3), small(1), small(2), small(3)
        if k == 1:
            act(T.yw[:, 0:512:32], T.jr[:, 0:16], ["jr0", "tg", "yw"], ["yc0"], bias=turned(5), grp="yc")
            act(T.yw[:, 16:512:32], T.jr[:, 0:16], ["jr0", "tg", "yw"], ["yc1"], bias=turned(5), grp="yc")
            tt(x2(0, 1, 8, 16), T.tq[:, 16:24], x2(1, 1, 8, 16), A.subtract, ["xh0", "xc"], ["xj0"], "xj")
            tt(x2(0, 1, 16, 24), T.tq[:, 16:24], T.tq[:, 24:32], A.subtract, ["xh0", "xc"], ["xj1"], "xj")
        quant(half(q, 1), half(p, 1), T.vt[:], ["vt%d" % b for b in range(4)], ["q%d1" % k])
        send(k, raw(half(q, 0)), raw(half(q, 1)), "rq%d" % k, ["q%d1" % k])
        if k == 3:
            send(k, half(p, 0), half(p, 1), "rp%d" % k, ["q%d1" % k])
        arrive(k, "ri%d" % k, ["iw%d0" % k])
        arrive(k, "rq%d" % k, ["aq%d" % k])
        arrive(k, "rp%d" % k, ["ap%d" % k])

        def relist():
            for h in range(2):
                for t in range(2):
                    ts(T.yw[:, 256 * h + 1 + t:256 * h + 256:16], iw[:, 32 * h + 16 * t:32 * h + 16 * t + 16],
                       (16.0, 1.0, 0.0625)[k - 1] if t else 1.0, None, A.mult, None,
                       ["iw%d%d" % (k, h), "yw"], ["ya%d%d" % (h, t)], "y%d" % k)
            tr(T.ty[:], T.yw[:], ["ya00", "yw", "yc0"], ["ty"])

        if k < 3:
            c0, cr = 64 * k - 64, T["cr%d" % k]
            scores(k, 1, 0, ["q%d1" % k])
            total(1, half(q, 1), half(p, 1), 128, ["q%d1" % k])
            act(T.cs[:, c0 + 2:c0 + 64:4], T.rn[:, 0:16], ["sm", "cs"], ["ct%d" % k], scale=0.0, bias=T.sm[:])
            act(T.hi[:], T.jt[:, 48:64], ["jt3", "sm"], ["hi"], scale=2.0, bias=T.sm[:])
            if k == 1:
                ts(x2(0, 1, 0, 8), near, turned(3), -2.0, A.is_gt, A.mult, ["tg", "xc"], ["xk"])
                thresholds(4, col(4), ["cg"])
                quant(half(T.qx, 1), half(T.px, 1), T.xc[:], ["xc", "xh0", "xj0", "xk"], ["qx1"])
            for b in range(2):
                unpack(b, 4 + b, half(q, 1), half(p, 1), 128, ["q%d1" % k])
            flags("fl%d" % k, 0, 0, 4)
            count(1)
            for b in range(2, 4):
                unpack(b, 4 + b, half(q, 1), half(p, 1), 128, ["q%d1" % k])
            if k == 1:
                ts(T.so[:], T.jr[:, 112:128], turned(6), None, A.add, None, ["jr6", "th"], ["so"])
                quant(T.qv[:], T.pv[:], T.vs[:], ["vs"], ["qv"])
            cp(T.cs[:, c0 + 1:c0 + 64:2], bank[2][:, 64:96], ["b2", "cs"], ["cs%d" % k])
            send(k, cr[:], T.cs[:, c0:c0 + 64], "rc%d" % k, ["cs%d" % k, "ct%d" % k])
            send(k, half(p, 0), half(p, 1), "rp%d" % k, ["q%d1" % k])
            arrive(k, "rc%d" % k, ["cr%d" % k])
            for b in range(4):
                keep(b, 4 + b, T.fh, 128, 128, ["f%d1"])
            tt(T.own[:, 0:64:4], bank[2][:, 32:64:2], T.hi[:], A.add, ["b2", "hi"], ["own0"])
            cp(T.own[:, 2:64:4], bank[2][:, 33:64:2], ["b2"], ["own2"])
            relist()
            act(T.src[:], T.ty[:].indirect(T.so[:]), ["ty", "so"], ["src"])
            if k == 1:
                ts(T.fo[:], T.jr[:, 0:16], 0.5, turned(7), A.mult, A.add, ["jr0", "th"], ["fo"])
                ts(T.lo[:], T.jr[:, 32:48], turned(8), None, A.add, None, ["jr2", "th"], ["lo"])
            for b in range(4):
                unpack(b, 4 + b, half(q, 0), half(p, 0), 128, ["aq%d" % k, "ap%d" % k])
                keep(b, 4 + b, T.fh, 0, 128, ["f%d0"])
            scan(T.sc[:], cr[:], T.own[:], ["own0", "own1", "own2", "cr%d" % k], ["sc"])
        else:
            mm(bank[0][:, 0:128], T.qv[:], T.pv[:], half(q, 1), half(p, 1), ["qv", "q31"], ["b0"])
            relist()
            cp(T.yo[:, 1:256:2], bank[0][:, 0:128], ["b0"], ["yo1"])
            act(T.lro[:], T.ty[:].indirect(T.lo[:]), ["ty", "lo"], ["lro"])
            dma("y", T.lr[:, 0:256], T.lro[1:128:16, :], ["lro"], ["o0"], "out0")
            dma("y", T.lr[:, 256:512], T.lro[2:128:16, :], ["lro"], ["o1"], "out0")
            mm(bank[1][:, 0:128], T.qv[:], T.pv[:], half(q, 0), half(p, 0), ["qv", "aq3", "ap3"], ["b1"])
            for h in range(2):
                cp(words(half(T.qf, h)), words(q[:]).indirect(T.fo[:, 8 * h:8 * h + 8]), ["aq3", "q31", "fo"], ["qf%d" % h])
                dma("y", T.oc[:, 512 * h:512 * h + 512], raw(half(T.qf, h)), ["qf%d" % h], ["o2%d" % h], "out1")
            act(T.pf[:], p[:].indirect(T.fo[:]), ["ap3", "q31", "fo"], ["pf"])
            cp(T.yo[:, 0:256:2], bank[1][:, 0:128], ["b1"], ["yo0"])
            dma("y", T.y[:], T.yo[:], ["yo0", "yo1"], ["o3"], "out1")
            for j in range(4):
                dma("sssy"[j], T.osc[4 * j:4 * j + 4, :], T.pf[32 * j:32 * j + 4, :], ["pf"], ["o4%d" % j], "out2")
    op("y", None, ["o0", "o3", "o40"], [])
    emit(ops, queues, T)
    g.wait_ge(T.sem.sent, sent[0])
